import numpy as np, ml_dtypes
CORES = [25,29,65,69,153,157,193,197]
N = 8
import mx_ref
BF = ml_dtypes.bfloat16
def gentries(a):
    return np.ascontiguousarray(a.reshape(8, 16, -1).transpose(0, 2, 1)).reshape(8, -1)
def gtable(e):
    e = np.asarray(e); return np.ascontiguousarray(e.reshape(8, -1, 16).transpose(0, 2, 1)).reshape(128, -1).astype(np.int32)
def gcols(t, e):
    v = np.concatenate([t.reshape(8, 16, -1, 4), np.zeros((8, 16, 1, 4), BF)], axis=2)
    return np.ascontiguousarray(np.stack([v[g][:, e[g]] for g in range(8)])).reshape(128, -1)
def tile(rs):
    return np.stack(rs, axis=2).reshape(128, -1).astype(BF)
def pick(q, e):
    c = np.concatenate([q[0].reshape(128, -1, 4), np.zeros((128, 1, 4), np.uint8)], axis=1); s = np.concatenate([q[1], np.ones((16, 1), np.uint8)], axis=1)
    return (np.ascontiguousarray(c[:, e].reshape(128, -1)), np.ascontiguousarray(s[:, e]))
def join(*qs):
    return (np.concatenate([q[0] for q in qs], axis=1), np.concatenate([q[1] for q in qs], axis=1))
def put(q, e, v):
    c, s = q[0].reshape(128, -1, 4).copy(), q[1].copy(); c[:, e] = v[0].reshape(128, -1, 4); s[:, e] = v[1]
    return (c.reshape(128, -1), s)
def pk(c, s):
    return (np.ascontiguousarray(c), mx_ref.live(s))
def emit(q):
    return q[0], q[1]
def packed(v, rng):
    q = [mx_ref.quantize(np.ascontiguousarray(v[r])) for r in range(N)]
    return np.stack([a for a, b in q]), np.stack([mx_ref.plane(b, rng) for a, b in q])
def values_of_codes():
    e, c = np.zeros((128, 128, 4), np.float32), np.zeros((128, 2, 4), np.uint8)
    e[np.arange(128), np.arange(128), 0] = 1
    c[:127, :, 0] = np.arange(256).reshape(2, 128).T[:127]
    return mx_ref.matmul(mx_ref.quantize(e.reshape(128, 512).astype(BF)), (c.reshape(128, 8), np.full((16, 2), 127, np.uint8))).T.reshape(-1).astype(np.float64)
CODE_VALUE, SCALE_VALUE = values_of_codes(), 2.0 ** (np.arange(256) - 127.0)
def decode(q):
    return (CODE_VALUE[q[0]].reshape(16, 8, -1, 4) * SCALE_VALUE[q[1]][:, None, :, None] + 0.0).reshape(128, -1).astype(np.float32)
def f(rng, *shape):
    return mx_ref.flush((rng.standard_normal(shape, dtype=np.float32) * np.exp2(rng.integers(-2, 3, shape[:-1] + (1,)))).astype(BF))
def wide(rng, *shape, cols=0):
    v = rng.standard_normal(shape, dtype=np.float32) * np.exp2(rng.integers(-12, 13, shape)).astype(np.float32)
    if cols: v *= np.repeat(np.exp2(rng.integers(-cols, cols + 1, shape[:-2] + (1, shape[-1] // 4))) * (rng.random(shape[:-2] + (1, shape[-1] // 4)) > 0.0625), 4, axis=-1).astype(np.float32)
    return mx_ref.flush(v.astype(BF))
C, L, M, R = 320, 32, 160, 3
STEP = [1, 2, 4]
place = np.arange(C)
def at(a, e):
    return np.take_along_axis(a, e, axis=1)
def big(v):
    v = v.astype(np.float32)
    v[np.abs(v) < np.float32(2.0 ** -16)] = 0
    return v.astype(BF)
def numbers_of(rng):
    return {"x": big(f(rng, N, 128, 4 * C)), "u": np.array(f(rng, N, 128, 512)), "v": np.array(f(rng, N, 128, 512))}
def layers(rng):
    return big(f(rng, N, 128, 2048)).reshape(N, 8, 16, 4, 8, 16, 4)
def weights(rng, w):
    c, p = packed(np.ascontiguousarray(w).reshape(N, 128, 2048), rng)
    return {"wc": c, "ws": p}
def twins(rng):
    o = np.argsort(rng.random((N, 8, C)), axis=2)
    e = np.zeros((N, 8, C), int)
    np.put_along_axis(e, o[:, :, :M], o[:, :, M:], axis=2)
    np.put_along_axis(e, o[:, :, M:], o[:, :, :M], axis=2)
    return e
def listed(e):
    return {"tw": np.stack([gtable(e[r]) for r in range(N)])}
def signs(rng):
    return np.stack([rng.permutation(8) % 2 * 2.0 - 1.0 for r in range(N)])
def setup_inputs(rng):
    return {**numbers_of(rng), **weights(rng, layers(rng)), **listed(twins(rng))}
def setup_inputs_ties(rng):
    d = numbers_of(rng)
    e = rng.permutation(N)
    x = d["x"].reshape(N, 8, 16, C, 4)
    for r in range(N):
        k = np.zeros(C, int) if r == e[0] else rng.permutation(C) % 3
        a = x[r][:, :8, :3].copy()
        a[:, :, 2] = 0
        x[r][:, :8] = a[:, :, k]
    x[e[1]] = 0
    u = d["u"].reshape(N, 8, 16, 8, 16, 4)
    k = u.copy()
    u[:, :, :, :, 0] = 0
    for g in range(8): u[:, g, :8, g, 0] = k[:, g, :8, g, 0]
    w = layers(rng)
    w[:, :, :, :, :, :8] = 0
    return {"x": x.reshape(N, 128, 4 * C), "u": u.reshape(N, 128, 512), "v": d["v"], **weights(rng, w), **listed(twins(rng))}
def setup_inputs_near(rng):
    d = numbers_of(rng)
    x = np.zeros((N, 8, 16, C, 4), np.float32)
    u = d["u"].reshape(N, 128, 128, 4)
    u[:, :, ::16] = 0
    o, e = rng.permutation(N) % 4, twins(rng)
    n = np.arange(M)
    for r in range(N):
        size = 1.0 if o[r] < 2 else 2.0 ** -4
        k = 1.0 if o[r] == 0 else 2.0 ** -30
        kind = rng.permutation(8)
        for g in range(8):
            low = np.flatnonzero(place < e[r, g])
            high = e[r, g][low]
            h, c = 16 * g, 1.0 - 2.0 * (kind[g] % 2)
            u[r, h, h, 0] = k
            u[r, h + 8:h + 12, h] = k
            s, unit = np.zeros(C, int), 2.0 ** -23 * size
            if kind[g] < 4:
                i = (n + rng.integers(0, (M - L) // 2 + 1)) % M
                upper = i // (M // 2)
                more = (M - i) // 2 + 1 if o[r] < 2 else M // 2 - i % (M // 2) + 1 - upper
                s[low] = rng.integers(0, 255 - M // 2, M)
                s[high] = s[low] + more
                if o[r] < 2:
                    u[r, h, h, 0] = k * 2.0 ** 20
                    x[r, g, 0, :, 0] = c * 2.0 ** -20
                    j = int(np.argmax(more))
                    if kind[g] < 2: x[r, g, 0, high[j] if c > 0 else low[j], 0] *= np.float32(2.0 ** 50)
                else:
                    x[r, g, 0, :, 0] = 8 * 2.0 ** -30
                    x[r, g, 0, high[upper == 0], 0] = 9 * 2.0 ** -30
            elif o[r] < 2:
                great, small = (high, low) if c > 0 else (low, high)
                third = 3 * n // M
                s[small] = 512 * (2 * int(rng.integers(17, 32)) - (third == 0)) + 255 * (third != 1)
                x[r, g, 0, great, 0] = 512 * c
                x[r, g, 0, small, 0] = 0.5 * c
                unit = 2.0 ** -24 * c
            else:
                m = np.where(n < M // 2, 10, 9) * 2.0 ** -32
                x[r, g, :2, :, 0] = 8 * 2.0 ** -32
                x[r, g, 0, high, 0] = m
                x[r, g, 1, low, 0] = m
                u[r, h, h, 0] = 9 * 2.0 ** -33
                u[r, h + 1, h, 0] = 2.0 ** -30
            z = ((s[:, None] >> np.arange(16)) & 1) * np.exp2(np.arange(16.0)) * unit + 0.0
            for i in range(4): x[r, g, 8 + i] = z[:, 4 * i:4 * i + 4]
        x[r, :, 12:] = rng.integers(4, 8, (8, 4, C, 4)) * 2.0 ** -20 * size
    w = layers(rng)
    w[:, :, :12] = 0
    w[:, :, :, :, :, :12] = 0
    return {"x": x.reshape(N, 128, 4 * C).astype(BF), "u": u.reshape(N, 128, 512), "v": d["v"], **weights(rng, w), **listed(e)}
def setup_inputs_arcs(rng):
    d = numbers_of(rng)
    x = d["x"].astype(np.float32).reshape(N, 8, 16, C, 4)
    u = d["u"].reshape(N, 128, 128, 4)
    u[:, :, ::16] = 0
    size = np.where(rng.permutation(N) < N // 2, 2.0 ** -30, 1.0).astype(np.float32).astype(BF)
    e = np.zeros((N, 8, C), int)
    for r in range(N):
        k, m, n = rng.permutation(8), rng.permutation(8), rng.permutation(8)
        for g in range(8):
            ways = [place, place[::-1], np.argsort(place % 2, kind="stable"), np.argsort(-(place % 2), kind="stable"), np.roll(place, M // 2), np.roll(place, int(rng.integers(1, C))), rng.permutation(C), rng.permutation(C)]
            low = np.sort(ways[k[g]][:M])
            high = np.setdiff1d(place, low)
            if m[g] % 3 == 1: high = high[::-1]
            if m[g] % 3 == 2: high = rng.permutation(high)
            more = [np.arange(1, M + 1), np.arange(M, 0, -1), np.ones(M, int), rng.permutation(M) + 1][n[g] % 4]
            key = np.zeros(C, int)
            key[low] = rng.integers(0, 256, M)
            key[high] = key[low] + more
            z = ((key[:, None] >> np.arange(12)) & 1) * np.exp2(np.arange(12.0))
            for i in range(3): x[r, g, 8 + i] = z[:, 4 * i:4 * i + 4]
            e[r, g, low] = high
            e[r, g, high] = low
        for h in range(0, 128, 16): u[r, h + 8:h + 11, h] = size[r]
    w = layers(rng)
    w[:, :, 8:11] = 0
    w[:, :, :, :, :, 8:11] = 0
    return {"x": x.reshape(N, 128, 4 * C).astype(BF), "u": u.reshape(N, 128, 512), "v": d["v"], **weights(rng, w), **listed(e)}
def setup_inputs_huge(rng):
    d = numbers_of(rng)
    e = twins(rng)
    c = np.ones((N, C))
    x = 0.7 + 0.2 * rng.random((N, 128, C, 4))
    a = 1 - 0.1 * rng.random((N, 128, 8, 4))
    for r in rng.permutation(N)[:N // 2]:
        x[r] = 0.9375 - 0.1 * rng.random((128, C, 4)) ** 4
        a[r] = 1 - 0.025 * rng.random((128, 8, 4))
        a[r, :, :, 0] = 1
        c[r] = rng.permutation(C) % 2 * 2.0 - 1.0
        for g in range(8):
            i, j = rng.permutation(np.flatnonzero(c[r] > 0)), np.flatnonzero(c[r] < 0)
            e[r, g, i] = j
            e[r, g, j] = i
    x = 2.0 ** 30 * x * c[:, None, :, None]
    u = d["u"].reshape(N, 128, 128, 4)
    a = 2.0 ** 30 * a * signs(rng)[:, None, :, None]
    u[:, :, ::16] = a.astype(np.float32).astype(BF)
    w = np.zeros((N, 128, 4, 128, 4), np.float32)
    i = np.arange(128)
    for b in range(4): w[:, i, b, i, b] = -0.25
    return {"x": x.astype(np.float32).reshape(N, 128, 4 * C).astype(BF), "u": u.reshape(N, 128, 512), "v": d["v"], **weights(rng, w.astype(BF)), **listed(e)}
def setup_inputs_spread(rng):
    d = setup_inputs(rng)
    d["x"] = big(wide(rng, N, 128, 4 * C, cols=6))
    return d
def check_inputs(d):
    b = []
    for k in ("x", "u", "v"):
        a = np.abs(d[k].astype(np.float32))
        if not (np.isfinite(a).all() and ((a == 0) | (a >= 2.0 ** -30) & (a <= 2.0 ** 30)).all()): b.append("a value of " + k)
    none, least, most = [emit(mx_ref.quantize(np.full((128, 16), k, np.float32).astype(BF)))[1][0, 0] for k in (0.0, 2.0 ** -30, 2.0 ** 30)]
    for r in range(N):
        if ((d["wc"][r] == 0x7F) | (d["wc"][r] == 0xFF)).any(): b.append("wc: a code that is no number")
        s = mx_ref.live(d["ws"][r])
        if ((s != none) & ((s < least) | (s > most))).any(): b.append("ws: a scale out of range")
        e = gentries(d["tw"][r])
        if ((e < 0) | (e >= C)).any(): b.append("tw: a twin out of range")
        elif (e == place).any() or (at(e, e) != place).any(): b.append("tw: places that aren't each other's twins")
    return b
def reference(x, u, v, wc, ws, tw):
    qu = [mx_ref.quantize(u[r]) for r in range(N)]
    lay = [pk(wc[r], ws[r]) for r in range(N)]
    now = [x[r] for r in range(N)]
    twin = [gentries(tw[r]) for r in range(N)]
    for t in range(R):
        kept, sent, named = [], [], []
        for r in range(N):
            e = twin[r]
            s = mx_ref.matmul(qu[r], mx_ref.quantize(now[r]))[::16] + np.float32(0.0)
            o = np.argsort(~((s < at(s, e)) | (s == at(s, e)) & (place > e)), axis=1, kind="stable")[:, :M]
            a = (np.stack([np.searchsorted(o[g], place, "right") for g in range(8)]) - 1) % M
            over = at(e, o)
            z = ((gcols(now[r], np.roll(o, 1, axis=1)).astype(np.float32) + gcols(now[r], at(o, at(a, over))).astype(np.float32)) * np.float32(0.5)).astype(BF)
            q = mx_ref.quantize(z)
            h = tile([mx_ref.matmul(pick(lay[r], np.arange(128 * b, 128 * b + 128)), q) * np.float32(0.03125) for b in range(4)])
            new = (now[r].astype(np.float32) + gcols(h, a).astype(np.float32)).astype(BF)
            weak = np.argsort(at(s, over) - at(s, o), axis=1, kind="stable")[:, :L]
            gone = np.zeros((8, C), bool)
            np.put_along_axis(gone, np.concatenate([at(o, weak), at(over, weak)], axis=1), True, axis=1)
            i = np.argsort(gone, axis=1, kind="stable")
            named.append(at(np.argsort(i, axis=1), at(e, i)))
            kept.append(gcols(new, i[:, :C - 2 * L]))
            sent.append(gcols(decode(mx_ref.quantize(new)).astype(BF), i[:, C - 2 * L:]))
        for r in range(N):
            p = (r - STEP[t]) % N
            now[r] = np.concatenate([kept[r], sent[p]], axis=1)
            twin[r] = np.concatenate([named[r][:, :C - 2 * L], named[p][:, C - 2 * L:]], axis=1)
    y, ot = np.zeros((N, 128, C), np.float32), np.zeros((N, 8, C), np.float32)
    oc, osc = np.zeros((N, 128, 4 * C), np.uint8), np.zeros((N, 16, C), np.uint8)
    for r in range(N):
        q = mx_ref.quantize(now[r])
        y[r] = mx_ref.matmul(mx_ref.quantize(v[r]), q)
        ot[r] = twin[r]
        oc[r], osc[r] = emit(q)
    return {"y": y, "ot": ot, "oc": oc, "osc": osc}

@@ -1,0 +1,681 @@
+import numpy as np
+from concourse.bass import DstId, RemoteDMATransfer
+from concourse.mybir import dt, AluOpType, AxisListType, ActivationFunctionType
+
+A = AluOpType
+F = ActivationFunctionType
+C, M, R, STAY, GO = 320, 160, 3, 256, 64
+STEP = [1, 2, 4]
+TINY = 2.0 ** -120
+UP, DOWN = 1024.0, -33792.0
+HW = 176
+f32, b16, i32, u16, q8, u8 = "float32", "bfloat16", "int32", "uint16", "float8_e4m3fn_x4", "uint8"
+
+PER = {"s": (320, f32), "tie": (320, f32), "dd": (320, f32), "nu": (320, b16), "cnt": (320, b16), "aT": (320, b16),
+       "sA": (320, f32), "aD": (32, u16), "acc": (32, f32), "ac2": (32, f32), "oD": (16, u16), "lD": (16, u16),
+       "qD": (16, u16), "gab": (320, f32), "sab": (320, f32), "ab4": (80, u16), "dR": (160, f32), "dm": (160, f32),
+       "dsc": (160, f32), "df": (160, f32), "XO": (656, b16), "XA": (656, b16), "sT": (320, f32), "Z": (656, b16),
+       "H": (4 * HW, b16), "E": (1280, b16), "fl": (176, b16), "nst": (8, f32), "lu": (320, b16), "luT": (320, b16),
+       "luN": (320, b16), "cl": (320, b16), "cs": (320, b16), "clT": (320, b16), "csT": (320, b16), "lw": (64, f32),
+       "slw": (64, f32), "twn": (256, f32), "stw": (256, f32), "qz": (176, q8), "sz": (176, u8), "qc": (480, q8), "sc": (480, u8)}
+JUNK = {"o0": (0, 10, 176), "op": (1780, 8, 144), "on": (2948, 2, 64), "l": (3080, 4, 320), "q": (4368, 16, 80)}
+ONE = {"x0": (1280, b16), "ut": (512, b16), "vt": (512, b16), "twi": (20, i32), "wq": (512, q8), "wp": (512, u8),
+       "qu0": (128, q8), "su0": (128, u8), "qu": (128, q8), "su": (128, u8), "qv": (128, q8), "sv": (128, u8),
+       "iota": (320, f32), "iotT": (320, f32), "iotU": (320, f32), "far": (512, f32), "sg": (1600, b16),
+       "j16": (320, f32), "j4": (320, f32), "ge": (512, b16), "pi": (8, i32),
+       "pk": (8, i32), "col": (16, f32), "c16": (20, f32), "kb": (20, f32), "ob": (20, f32), "urep": (8, u16), "blk": (16, u16),
+       "mask": (320, f32), "sel16": (320, f32), "m4": (320, f32), "sel4": (320, f32), "rst": (160, f32), "eps": (160, f32),
+       "ones": (512, b16), "bd": (512, b16), "qbd": (128, q8), "sbd": (128, u8), "eb": (2048, b16),
+       "qe": (512, q8), "se": (512, u8), "zero": (640, b16), "qdump": (128, q8), "CC": (1920, b16), "L": (512, b16),
+       "yb": (320, f32), "otb": (320, f32), "junk": (5680, b16)}
+for _t in range(R + 1):
+    ONE["qx%d" % _t] = (320, q8)
+    ONE["sx%d" % _t] = (320, u8)
+    ONE["tw%d" % _t] = (32, u16)
+for _t in range(R):
+    ONE["x%d" % (_t + 1)] = (1280, b16)
+    ONE["ql%d" % _t] = (128, q8)
+    ONE["sl%d" % _t] = (256, u8)
+    ONE["wl%d" % _t] = (8, u16)
+    ONE["lc%d" % _t] = (192, q8)
+    ONE["ls%d" % _t] = (384, u8)
+for _t in range(2):
+    ONE["rc%d" % _t] = (64, q8)
+    ONE["rs%d" % _t] = (256, u8)
+    ONE["rl%d" % _t] = (8, u16)
+SCRATCH = {k: ("sbuf", [128, w * R], d) for k, (w, d) in PER.items()}
+SCRATCH.update({k: ("sbuf", [128, w], d) for k, (w, d) in ONE.items()})
+SCRATCH["ps"] = ("psum", [128, 4096], f32)
+DTYPE = {k: v[2] for k, v in SCRATCH.items()}
+NDMA = 24
+SEMAPHORES = (["V", "S", "P", "G", "out"] + ["d%d" % i for i in range(NDMA)] + ["ad%d" % t for t in range(R)]
+              + ["al%d" % t for t in range(R)] + ["hd%d" % t for t in range(2)] + ["hl%d" % t for t in range(2)])
+
+LAT, HOP2, HOP1, DMA, GATHER = 80.0, 5000.0, 3000.0, 2200.0, 1.6
+TRIES = 4000
+
+
+def route(t, r, T, topo):
+    n = len(T.cores)
+    src, dst = T.cores[r], T.cores[(r + STEP[t]) % n]
+    if topo.may_write(src, dst):
+        return dst, None
+    can = [c for c in topo.cores_of(src) if T.rank_of(c) is None and topo.may_write(c, dst)]
+    near = [c for c in can if topo.die(c) == topo.die(src)]
+    far = [c for c in can if topo.die(c) != topo.die(src)]
+    alone = all(topo.may_write(c, T.cores[(T.rank_of(c) + STEP[t]) % n]) for c in topo.cores_of(src) if c != src and T.rank_of(c) is not None)
+    return dst, (near[0], near[1], far[:2] if alone else [near[1]])
+
+
+def masks(src, dst, parts, topo):
+    e = topo.engines(src, dst)
+    k = len(e) // parts
+    return [sum(1 << x for x in e[i * k:(i + 1) * k]) for i in range(parts)], k
+
+
+def did(dst, src, topo):
+    rid, pid = topo.addr(dst, src)
+    return DstId(rid=rid, pnc=pid)
+
+
+def relay_program(g, core, T, topo):
+    total = 0
+    for t in range(2):
+        for r in range(len(T.cores)):
+            dst, via = route(t, r, T, topo)
+            if via is None or (core not in via[:2] and core not in via[2]):
+                continue
+            src = T.cores[r]
+            rid, pid = topo.addr(dst, core)
+            m, k = masks(core, dst, 1, topo)
+            if core in via[:2]:
+                g.wait_ge(T.sem["hd%d" % t], masks(src, core, 2, topo)[1])
+                if core == via[0]:
+                    g.remote_dma(T["lc%d" % t][:, 128:192].bitcast(dt.uint8), T["rc%d" % t][:, 0:64].bitcast(dt.uint8), T.sem["ad%d" % t], T.sem.out, pid, rid, m[0])
+                else:
+                    g.remote_dma(T["ls%d" % t][:, 128:192], T["rs%d" % t][:, 0:64], T.sem["ad%d" % t], T.sem.out, pid, rid, m[0])
+                total += k
+            if core in via[2]:
+                w = 4 // len(via[2])
+                i = via[2].index(core)
+                g.wait_ge(T.sem["hl%d" % t], masks(src, core, len(via[2]), topo)[1])
+                g.remote_dma(T["tw%d" % (t + 1)][:, 16 + i * w:16 + (i + 1) * w], T["rl%d" % t][:, 0:w], T.sem["al%d" % t], T.sem.out, pid, rid, m[0])
+                total += k
+    if total:
+        g.wait_ge(T.sem.out, total)
+
+
+def plan():
+    ops = []
+
+    def v(name, lo, hi, step=1, t=None):
+        if name in PER:
+            lo, hi = lo + t * PER[name][0], hi + t * PER[name][0]
+        return (name, lo, hi, step)
+
+    def size(a):
+        if a[0] == "ind":
+            return 16 * (a[2][2] - a[2][1])
+        return len(range(a[1], a[2], a[3]))
+
+    def regs(xs):
+        out = []
+        for a in xs:
+            if not isinstance(a, tuple):
+                continue
+            if a[0] == "ind":
+                out += [a[1], a[2]]
+            else:
+                out.append(a)
+        return out
+
+    def add(alts, reads, writes, **kw):
+        rd, wr = [], list(regs(writes))
+        for a in regs(reads):
+            (wr if a[0] == "ps" else rd).append(a)
+        wr = [("ps", a[1] // 512 * 512, (a[2] + 511) // 512 * 512, 1) if a[0] == "ps" else a for a in wr]
+        ops.append(dict(alts=alts, rd=rd, wr=wr, **kw))
+
+    def two(*xs):
+        return all(DTYPE[a[0]] in (b16, u16) for a in xs)
+
+    def vc(n, c=1.0):
+        return 50.0 + max(64.0, n * c)
+
+    def vcost(out, a, c=1.0):
+        if a[0] == "ind":
+            return 50.0 + GATHER * size(a)
+        return vc(size(a), c * (0.5 if two(out, a) else 1.0))
+
+    def scost(a):
+        return 65.0 + (GATHER * size(a) if a[0] == "ind" else max(64.0, size(a)))
+
+    def ts(out, a, s1, s2, op0, op1=None):
+        add([("V", vcost(out, a), ("ts", out, a, s1, s2, op0, op1))], [a, s1, s2], [out])
+
+    def tt(out, a, b, op):
+        add([("V", vcost(out, a, 1.0 if b[0] == "ps" else 2.0), ("tt", out, a, b, op))], [a, b], [out])
+
+    def scan(out, a, b, init, op0, op1):
+        add([("V", vc(size(a), 0.5 if two(out, a, b) else 1.0), ("scan", out, a, b, init, op0, op1))], [a, b, init], [out])
+
+    def lin(out, a, scale=1.0, bias=0.0):
+        if scale == 1.0 and bias == 0.0:
+            vo = ("copy", out, a)
+        elif bias == 0.0:
+            vo = ("ts", out, a, scale, None, A.mult, None)
+        else:
+            vo = ("ts", out, a, scale, bias, A.mult, A.add)
+        add([("S", scost(a), ("act", out, a, F.Identity, bias, scale, None)), ("V", vcost(out, a), vo)], [a], [out])
+
+    def act(out, a, func, bias, scale):
+        add([("S", scost(a), ("act", out, a, func, bias, scale, None))], [a, bias], [out])
+
+    def copy(out, a):
+        add([("V", vcost(out, a), ("copy", out, a))], [a], [out])
+
+    def fill(out, c):
+        add([("V", vc(size(out), 0.5 if two(out) else 1.0), ("memset", out, c))], [], [out])
+
+    def quant(q, s, a):
+        add([("V", 50.0 + 0.22 * size(a), ("quant", q, s, a))], [a], [q, s])
+
+    def mm(bank, w, wsc, x, xsc, start=True, stop=True):
+        n = size(x)
+        out = ("ps", 512 * bank, 512 * bank + n, 1)
+        add([("P", 60.0 + 0.7 * (n + 16), ("mm", out, w, wsc, x, xsc, start, stop))], [w, wsc, x, xsc], [out], acc=not start)
+
+    def iota(out, pattern, base, cm):
+        add([("G", 130.0 + 2.0 * size(out), ("iota", out, pattern, base, cm))], [], [out])
+
+    def dma(q, kind, reads, writes, *args):
+        add([(q, 100.0, (kind,) + args)], reads, writes, dma=True)
+
+    def ind(w, o):
+        return ("ind", w, o)
+
+    def ps(bank, lo, hi, step=1):
+        return ("ps", 512 * bank + lo, 512 * bank + hi, step)
+
+    dma("Y", "load", [], [v("x0", 0, 1280)], "x0", "x")
+    dma("S", "load", [], [v("ut", 0, 512)], "ut", "u")
+    dma("S", "load", [], [v("twi", 0, 20)], "twi", "tw")
+    dma("Y", "load", [], [v("wq", 0, 512)], "wq", "wc")
+    dma("Y", "load", [], [v("wp", 0, 512)], "wp", "ws")
+    dma("Y", "load", [], [v("vt", 0, 512)], "vt", "v")
+    iota(v("c16", 0, 20), [[16, 20]], 0, 0)
+    iota(v("pi", 0, 1), [[1, 1]], 0, 1)
+    iota(v("iota", 0, 320), [[1, 320]], 0, 0)
+    iota(v("j16", 0, 320), [[0, 20], [1, 16]], 0, 0)
+    iota(v("j4", 0, 320), [[0, 80], [1, 4]], 0, 0)
+    iota(v("ge", 0, 512), [[1, 8], [0, 64]], 0, 0)
+    iota(v("ob", 0, 20), [[32, 20]], 0, 0)
+    copy(v("urep", 0, 8), v("c16", 0, 8))
+    ts(v("blk", 0, 10), v("c16", 0, 10), 15.0, None, A.add)
+    ts(v("pk", 0, 1), v("pi", 0, 1), 15, None, A.bitwise_and)
+    ts(v("pk", 1, 2), v("pi", 0, 1), 3, None, A.bitwise_and)
+    ts(v("pk", 2, 3), v("pi", 0, 1), 4, None, A.arith_shift_right)
+    ts(v("pk", 3, 4), v("pi", 0, 1), 2, 3, A.arith_shift_right, A.bitwise_and)
+    copy(v("col", 0, 4), v("pk", 0, 4))
+    r_, t_, g_, r4_ = [v("col", i, i + 1) for i in range(4)]
+    k16, k16m, k16l, k4 = [v("col", i, i + 1) for i in range(4, 8)]
+    ts(v("kb", 0, 20), v("c16", 0, 20), r_, 0.5, A.add, A.add)
+    lin(k16, r_, UP, -15.0 * UP)
+    lin(k16m, r_, UP, -15.0 * UP - 1.0)
+    lin(k16l, r_, UP, -15.0 * UP + STAY - 1.0)
+    ts(k4, r4_, 4.0 * UP, t_, A.mult, A.add)
+    lin(k4, k4, 1.0, -12.0 * UP)
+    lin(v("iotT", 0, 320), v("iota", 0, 320), TINY)
+    lin(v("iotU", 0, 320), v("iota", 0, 320), TINY)
+    ts(v("mask", 0, 320), v("j16", 0, 320), r_, None, A.is_equal)
+    lin(v("sel16", 0, 320), v("mask", 0, 320), DOWN, UP)
+    act(v("far", 0, 320), v("j4", 0, 320), F.Abs, r4_, -1.0)
+    act(v("m4", 0, 320), v("far", 0, 320), F.Relu, 1.0, -1.0)
+    lin(v("sel4", 0, 320), v("m4", 0, 320), DOWN, UP)
+    act(v("rst", 0, 160), v("j16", 0, 160), F.Sign, 0.0, 1.0)
+    ts(v("eps", 0, 160), v("j16", 0, 160), r_, TINY, A.subtract, A.mult)
+    fill(v("ones", 0, 512), 1.0)
+    fill(v("zero", 0, 640), 0.0)
+    act(v("far", 0, 512), v("ge", 0, 512), F.Abs, g_, -1.0)
+    act(v("bd", 0, 512), v("far", 0, 512), F.Relu, 1.0, -1.0)
+    quant(v("qbd", 0, 128), v("sbd", 0, 128), v("bd", 0, 512))
+    for b in range(4):
+        e = v("eb", 512 * b, 512 * b + 512)
+        add([("G", 1200.0, ("sel", e, v("ones", 0, 512), [[-1, 512]], b, 4))], [v("ones", 0, 512)], [e])
+        quant(v("qe", 128 * b, 128 * b + 128), v("se", 128 * b, 128 * b + 128), e)
+    for j in range(3):
+        dma("Y", "move", [v("zero", 0, 640)], [v("CC", 640 * j, 640 * j + 640)], v("CC", 640 * j, 640 * j + 640), v("zero", 0, 640))
+    dma("Y", "move", [v("zero", 0, 256)], [v("L", 256, 512)], v("L", 256, 512), v("zero", 0, 256))
+    fill(("fl", 0, R * 176, 176), 0.0)
+    for b in range(4):
+        lin(("Z", 644 + b, R * 656, 656), v("zero", 0, R))
+    for k, (at, n, w) in JUNK.items():
+        fill(v("junk", at + w, at + n * (w + 2), w + 2), -float(w))
+    for t in range(R):
+        quant(v("lc%d" % t, 0, 128), v("ls%d" % t, 0, 128), v("zero", 0, 512))
+        quant(v("qdump", 0, 128), v("sl%d" % t, 128, 256), v("zero", 0, 512))
+    quant(v("qu0", 0, 128), v("su0", 0, 128), v("ut", 0, 512))
+    add([("V", 260.0, ("pick", v("qu", 0, 128), v("qu0", 0, 128), v("urep", 0, 8)))], [v("qu0", 0, 128), v("urep", 0, 8)], [v("qu", 0, 128)])
+    add([("V", 260.0, ("copy", v("su", 0, 128), ind(v("su0", 0, 128), v("urep", 0, 8)))),
+         ("S", 270.0, ("plane", v("su", 0, 128), ind(v("su0", 0, 128), v("urep", 0, 8))))], [v("su0", 0, 128), v("urep", 0, 8)], [v("su", 0, 128)])
+    quant(v("qv", 0, 128), v("sv", 0, 128), v("vt", 0, 512))
+    copy(v("tw0", 0, 20), v("twi", 0, 20))
+
+    def count(t, row, kind, c0, base, slide, at, out):
+        j0, n, width = JUNK[kind]
+        for i in range(n):
+            c = c0 + i
+            lo, jk = base + (16 * c if slide else 0), j0 + i * (width + 2)
+            win, j, j1, a, kb = v(row, lo, lo + width, 1, t), v("junk", jk, jk + width), v("junk", jk, jk + width + 1), v("acc", at + i, at + i + 1, 1, t), v("kb", c, c + 1)
+            add([("S", 90.0 + max(64, width), ("act", j, win, F.Sign, kb, -1.0, a)),
+                 ("V", vc(width, 0.5) + LAT + vc(width), ("multi", [("ts", j, win, kb, 2.0, A.is_le, A.mult), None, ("red", a, j1)]))],
+                [win, kb, j1], [j, a])
+        a = v("acc", at, at + n, 1, t)
+        if slide:
+            tt(v("ac2", at, at + n, 1, t), a, v("ob", c0, c0 + n), A.add)
+            a = v("ac2", at, at + n, 1, t)
+        ts(v(out, c0, c0 + n, 1, t), a, 0.5, base + width / 2.0, A.mult, A.add)
+
+    def scores(t, a0, a1, w, wsc, out):
+        e = min(a0, a1 - 128)
+        q, s = v("qx%d" % t, e, a1), v("sx%d" % t, e, a1)
+        quant(q, s, v("x%d" % t, 4 * e, 4 * a1))
+        bank = 1 if a0 else 0
+        mm(bank, w, wsc, q, s)
+        lin(out, ps(bank, a0 - e, a1 - e))
+        return ps(bank, a0 - e, a1 - e)
+
+    def halves(t, out, win, lst, a0, a1):
+        mid = a0 + (a1 - a0) // 64 * 32 if a1 - a0 > 64 else a1
+        for lo, hi in ((a0, mid), (mid, a1)):
+            if hi > lo:
+                lin(v(out, lo, hi, 1, t), ind(win, v(lst, lo // 16, hi // 16)))
+
+    def places(t, a0, a1):
+        tw = v("tw%d" % t, a0 // 16, a1 // 16)
+        p = lambda n: v(n, a0, a1, 1, t)
+        w = lambda n: v(n, 0, a1, 1, t)
+        held = scores(t, a0, a1, v("qu", 0, 128), v("su", 0, 128), p("s"))
+        if t == 0 or a0:
+            tt(p("tie"), ind(v("iotT", 0, 320), tw), v("iotU", a0, a1), A.subtract)
+        else:
+            lin(p("tie"), ind(v("tie", 0, C, 1, t - 1), v("qD", 0, 16, 1, t - 1)))
+        halves(t, "sT", w("s"), "tw%d" % t, a0, a1)
+        tt(p("dd"), p("sT"), held, A.subtract)
+        tt(p("nu"), p("dd"), p("tie"), A.is_le)
+        scan(p("cnt"), v("ones", a0, a1), p("nu"), v("cnt", a0 - 1, a0, 1, t) if a0 else 0.0, A.add, A.subtract)
+        lin(p("aT"), ind(w("cnt"), tw))
+        scan(p("sA"), v("sel16", a0, a1), p("cnt"), 0.0, A.add, A.max)
+        ts(v("aD", a0 // 16, a1 // 16, 1, t), v("sA", a0 + 15, a1, 16, t), k16, None, A.add)
+
+    def crossings(t, k0, k1, a1, po, pb):
+        n = k1 - k0
+        if k0:
+            count(t, "cnt", "on", 8, STAY, False, 8, "oD")
+        else:
+            count(t, "cnt", "o0" if k1 == M else "op", 0, 0, True, 0, "oD")
+        o = v("oD", k0 // 16, k1 // 16, 1, t)
+        lin(v("gab", po, po + n, 1, t), ind(v("iota", 0, 320), o))
+        lin(v("gab", pb, pb + n, 1, t), ind(v("aT", 0, a1, 1, t), o))
+        for lo, wd in ([(min(po, pb), 2 * n)] if k0 else [(po, n), (pb, n)]):
+            scan(v("sab", lo, lo + wd, 1, t), v("sel4", 0, wd), v("gab", lo, lo + wd, 1, t), 0.0, A.add, A.max)
+            ts(v("ab4", lo // 4, (lo + wd) // 4, 1, t), v("sab", lo + 3, lo + wd, 4, t), 4.0, k4, A.mult, A.add)
+        h = n // 4 if n > 64 else n
+        for i in range(0, n, h):
+            lin(v("XO", 4 * (1 + k0 + i), 4 * (1 + k0 + i + h), 1, t), ind(v("x%d" % t, 0, 4 * a1), v("ab4", (po + i) // 4, (po + i + h) // 4, 1, t)), 0.5)
+        if k0:
+            lin(v("XA", 4 * (1 + k0), 4 * (1 + k1), 1, t), ind(v("x%d" % t, 0, 4 * a1), v("ab4", po // 4, (po + n) // 4, 1, t)), 0.5)
+        else:
+            for i in (0, n // 2):
+                lin(v("XA", 4 * (1 + i), 4 * (1 + i + n // 2), 1, t), v("XO", 4 * (1 + i), 4 * (1 + i + n // 2), 1, t))
+        dd = ind(v("dd", 0, a1, 1, t), o)
+        k = lambda nm: v(nm, k0, k1, 1, t)
+        lin(k("dR"), dd)
+        tt(k("dm"), dd, v("mask", k0, k1), A.mult)
+        scan(k("dsc"), v("rst", k0, k1), k("dm"), 0.0, A.mult, A.max)
+        if t == 1 and k0 == 0:
+            for j in range(2):
+                lin(v("CC", 640 * j + 512, 640 * j + 640), v("zero", 0, 128))
+        for c in range(k0 // 16, k1 // 16):
+            own, at = v("dsc", 16 * c + 15, 16 * c + 16, 1, t), 640 * (c // 4) + c % 4
+            row, sg = v("dR", 0, k1, 1, t), v("sg", 160 * c, 160 * c + k1)
+            vo, so, outs = [], [("act", sg, row, F.Sign, own, -1.0, None), None], []
+            if c:
+                outs.append(v("CC", at, at + 64 * c, 4))
+                vo.append(("ts", outs[-1], v("dR", 0, 16 * c, 1, t), own, None, A.is_gt, None))
+                so.append(("act", outs[-1], v("sg", 160 * c, 176 * c), F.Relu, 0.0, -1.0, None))
+            if 16 * c + 16 < k1:
+                outs.append(v("CC", at + 64 * c + 64, at + 4 * k1 - c % 4, 4))
+                vo.append(("ts", outs[-1], v("dR", 16 * c + 16, k1, 1, t), own, None, A.is_ge, None))
+                so.append(("act", outs[-1], v("sg", 176 * c + 16, 160 * c + k1), F.Sign, 1.0, -1.0, None))
+            add([("V", sum(vc(size(x)) for x in outs), ("multi", vo)),
+                 ("S", scost(row) + LAT + sum(scost(x) for x in outs), ("multi", so))], [row, own], outs + [sg])
+        tt(k("df"), ind(v("dsc", 0, k1, 1, t), v("blk", k0 // 16, k1 // 16)), k("dR"), A.subtract)
+        tt(v("CC", 1280 + 4 * k0 + 2, 1280 + 4 * k1, 4), k("df"), v("eps", k0, k1), A.is_lt)
+        for j in ([0, 1] if k0 == 0 else []) + ([2] if k1 == M else []):
+            q, s = v("qc", 160 * j, 160 * j + 160, 1, t), v("sc", 160 * j, 160 * j + 160, 1, t)
+            quant(q, s, v("CC", 640 * j, 640 * j + 640))
+            mm(6, v("qbd", 0, 128), v("sbd", 0, 128), q, s, j == 0, j == 2)
+
+    def rest(t, pb):
+        w = lambda nm, n=320: v(nm, 0, n, 1, t)
+        tw = v("tw%d" % t, 0, 20)
+        x = "x%d" % t
+        lin(v("XO", 0, 4, 1, t), v("XO", 640, 644, 1, t))
+        lin(v("XA", 0, 4, 1, t), v("XA", 640, 644, 1, t))
+        for lo, hi in ((0, 128), (128, 160)) if t else ((0, 160),):
+            tt(v("Z", 4 + 4 * lo, 4 + 4 * hi, 1, t), ind(w("XO", 644), v("ab4", (pb + lo) // 4, (pb + hi) // 4, 1, t)), v("XA", 4 * lo, 4 * hi, 1, t), A.add)
+        lin(v("Z", 0, 4, 1, t), v("Z", 640, 644, 1, t))
+        quant(w("qz", 162), w("sz", 162), w("Z", 648))
+        for b in range(4):
+            mm(2 + b, v("wq", 128 * b, 128 * b + 128), v("wp", 128 * b, 128 * b + 128), w("qz", 162), w("sz", 162))
+            lin(v("H", HW * b, HW * b + 161, 1, t), ps(2 + b, 0, 161), 0.03125)
+            tt(v("E", 320 * b, 320 * b + 320, 1, t), ind(v("H", HW * b, HW * b + 161, 1, t), w("aD", 20)), v(x, b, 1280, 4), A.add)
+        if t == 0:
+            ts(v("fl", 1, 161, 1, t), ps(6, 0, 160), 32.0, None, A.is_lt)
+        else:
+            ts(v("fl", 1, 129, 1, t), ps(6, 0, 128), 32.0, None, A.is_lt)
+            add([("V", vc(128), ("red", w("nst", 1), v("fl", 1, 129, 1, t)))], [v("fl", 1, 129, 1, t)], [w("nst", 1)])
+            ts(v("fl", 129, 161, 1, t), ps(6, 128, 160), w("nst", 1), 32.0, A.add, A.is_lt)
+        tt(w("lu"), ind(w("fl", 161), w("aD", 20)), w("nu"), A.is_gt)
+        halves(t, "luT", w("lu"), "tw%d" % t, 0, C)
+        scan(w("cl"), w("luT"), w("lu"), 0.0, A.add, A.add)
+        count(t, "cl", "l", 0, 0, False, 10, "lD")
+        l, q = w("lD", 4), w("qD", 16)
+        for b in range(4):
+            lin(v("L", b, 256, 4), ind(v("E", 320 * b, 320 * b + 320, 1, t), l))
+        quant(v("ql%d" % t, 0, 128), v("sl%d" % t, 0, 128), v("L", 0, 512))
+        add([("G", 600.0, ("sendd", t))], [v("ql%d" % t, 0, 64), v("sl%d" % t, 0, 256)], [("goneD%d" % t, 0, 1, 1)], send=True)
+        lin(w("clT"), ind(w("cl"), tw))
+        lin(w("lw", 64), ind(w("clT"), l))
+        scan(w("slw", 64), v("sel16", 0, 64), w("lw", 64), 0.0, A.add, A.max)
+        ts(v("wl%d" % t, 0, 4), v("slw", 15, 64, 16, t), k16l, None, A.add)
+        add([("G", 600.0, ("sendl", t))], [v("wl%d" % t, 0, 4), ("goneD%d" % t, 0, 1, 1)], [("goneL%d" % t, 0, 1, 1)], send=True)
+        lin(w("luN"), w("luT"), -1.0, 1.0)
+        scan(w("cs"), w("luN"), w("lu"), 0.0, A.add, A.subtract)
+        count(t, "cs", "q", 0, 0, True, 16, "qD")
+        nx = "x%d" % (t + 1)
+        for b in range(4):
+            lin(v(nx, b, 1024, 4), ind(v("E", 320 * b, 320 * b + 320, 1, t), q))
+        lin(w("csT"), ind(w("cs"), tw))
+        lin(w("twn", 256), ind(w("csT"), q))
+        scan(w("stw", 256), v("sel16", 0, 256), w("twn", 256), 0.0, A.add, A.max)
+        ts(v("tw%d" % (t + 1), 0, 16), v("stw", 15, 256, 16, t), k16m, None, A.add)
+
+    def arrive(t):
+        hop = HOP2 if t < 2 else HOP1
+        add([("N", hop, None)], [("goneL%d" % t, 0, 1, 1)], [v("tw%d" % (t + 1), 16, 20)], arrival="al%d" % t)
+        add([("N", hop, None)], [("goneD%d" % t, 0, 1, 1)], [v("lc%d" % t, 128, 192), v("ls%d" % t, 128, 384)], arrival="ad%d" % t)
+        for b in range(4):
+            mm(2 + b, v("qe", 128 * b, 128 * b + 128), v("se", 128 * b, 128 * b + 128), v("lc%d" % t, 64, 192), v("ls%d" % t, 64, 192))
+            lin(v("x%d" % (t + 1), 1024 + b, 1280, 4), ps(2 + b, 64, 128))
+
+    for t in range(R):
+        if t == 0:
+            places(t, 0, C)
+            crossings(t, 0, M, C, 0, 160)
+            rest(t, 160)
+        else:
+            places(t, 0, STAY)
+            crossings(t, 0, 128, STAY, 0, 128)
+            arrive(t - 1)
+            places(t, STAY, C)
+            crossings(t, 128, M, C, 288, 256)
+            rest(t, 128)
+    qv, sv = v("qv", 0, 128), v("sv", 0, 128)
+    scores(R, 0, 192, qv, sv, v("yb", 0, 192))
+    dma("Y", "codes", [v("qx3", 0, 192)], [], 0, 192)
+    dma("Y", "y", [v("yb", 0, 192)], [], 0, 192)
+    arrive(R - 1)
+    lin(v("otb", 0, C), ind(v("iota", 0, C), v("tw3", 0, 20)))
+    dma("Y", "ot", [v("otb", 0, C)], [])
+    scores(R, 192, C, qv, sv, v("yb", 192, C))
+    dma("Y", "codes", [v("qx3", 192, C)], [], 192, C)
+    for k in range(4):
+        dma("SY"[k % 2], "scales", [v("sx3", 0, C)], [], k)
+    dma("S", "y", [v("yb", 192, C)], [], 192, C)
+    return ops
+
+
+def meets(a, b):
+    if a[0] != b[0] or a[2] <= b[1] or b[2] <= a[1]:
+        return False
+    if a[3] == b[3] and a[3] > 1:
+        return a[1] % a[3] == b[1] % a[3]
+    return True
+
+
+def schedule(ops):
+    n = len(ops)
+    last = {}
+    for i, o in enumerate(ops):
+        deps = set()
+        for a in o["rd"]:
+            deps.update(j for (b, j, wr) in last.get(a[0], []) if wr and meets(a, b))
+        for a in o["wr"]:
+            deps.update(j for (b, j, wr) in last.get(a[0], []) if meets(a, b))
+        deps.discard(i)
+        o["deps"] = sorted(deps)
+        for a in o["rd"]:
+            last.setdefault(a[0], []).append((a, i, False))
+        for a in o["wr"]:
+            last.setdefault(a[0], []).append((a, i, True))
+    after = [[] for _ in range(n)]
+    for i, o in enumerate(ops):
+        for j in o["deps"]:
+            after[j].append(i)
+    extra = [DMA if o.get("dma") else 0.0 for o in ops]
+    least = [min(a[1] for a in o["alts"]) for o in ops]
+    ends = [i for i, o in enumerate(ops) if o.get("send")]
+
+    def attempt(weight, bias):
+        tail = [0.0] * n
+        for i in range(n - 1, -1, -1):
+            tail[i] = least[i] * weight[i] + extra[i] + max([LAT + tail[j] for j in after[i]] + [0.0])
+        busy = {e: [] for e in "VSPGY"}
+        done, got = [0.0] * n, [None] * n
+        for i in sorted(range(n), key=lambda x: -tail[x]):
+            o = ops[i]
+            at = max([done[j] + LAT for j in o["deps"]] + [0.0])
+            pick = None
+            for a in o["alts"]:
+                st, pos = at, 0
+                if a[0] != "N":
+                    for b0, b1 in busy[a[0]]:
+                        if st + a[1] <= b0:
+                            break
+                        if b1 > st:
+                            st = b1
+                        pos += 1
+                key = st + a[1] + (bias[i] if a[0] == "V" else 0.0)
+                if pick is None or key < pick[0]:
+                    pick = (key, a, st, pos)
+            key, a, st, pos = pick
+            if a[0] != "N":
+                busy[a[0]].insert(pos, (st, st + a[1]))
+            done[i] = st + a[1] + extra[i]
+            got[i] = (a, st)
+        return max(done) + 0.02 * sum(done[i] for i in ends), got, done
+
+    rng = np.random.default_rng(1)
+    weight, bias = np.full(n, 1.5), np.full(n, 300.0)
+    best = now = attempt(weight.tolist(), bias.tolist())
+    for it in range(TRIES):
+        w2, b2 = weight.copy(), bias.copy()
+        k = rng.random(n) < 0.004
+        w2[k] = np.exp(rng.normal(0.7, 0.8, int(k.sum())))
+        k = rng.random(n) < 0.004
+        b2[k] = rng.choice([-500.0, 0.0, 300.0, 1000.0, 5000.0], int(k.sum()))
+        new = attempt(w2.tolist(), b2.tolist())
+        if new[0] <= now[0] + 30.0 * (1.0 - it / TRIES):
+            now, weight, bias = new, w2, b2
+            if new[0] < best[0]:
+                best = new
+    for i, o in enumerate(ops):
+        a, st = best[1][i]
+        o["eng"], o["call"], o["start"], o["end"] = a[0], a[2], st, best[2][i]
+    return sorted(range(n), key=lambda i: (ops[i]["start"], i))
+
+
+PLAN = {}
+
+
+def rank_program(g, core, T, topo):
+    rank = T.rank_of(core)
+    if rank is None:
+        relay_program(g, core, T, topo)
+        return
+    if not PLAN:
+        PLAN["ops"] = plan()
+        PLAN["order"] = schedule(PLAN["ops"])
+    ops, order = PLAN["ops"], PLAN["order"]
+    n = len(T.cores)
+    queue = {"V": g.vector, "S": g.scalar, "P": g.tensor, "G": g, "Y": g.sync}
+
+    def ap(a):
+        if not isinstance(a, tuple):
+            return a
+        if a[0] == "ind":
+            return ap(a[1]).indirect(ap(a[2]))
+        return T[a[0]][:, a[1]:a[2]] if a[3] == 1 else T[a[0]][:, a[1]:a[2]:a[3]]
+
+    def arrivals(t):
+        src_rank = (rank - STEP[t]) % n
+        src = T.cores[src_rank]
+        via = route(t, src_rank, T, topo)[1]
+        if via is None:
+            k = len(topo.engines(src, core))
+            return k, k
+        return sum(len(topo.engines(c, core)) for c in via[2]), sum(len(topo.engines(c, core)) for c in via[:2])
+
+    sent = [0]
+
+    def send(kind, t):
+        dst, via = route(t, rank, T, topo)
+        tr = []
+        if kind == "sendl":
+            to = [dst] if via is None else via[2]
+            w = 4 // len(to)
+            for i, c in enumerate(to):
+                m, k = masks(core, c, len(to), topo)
+                out = T["tw%d" % (t + 1)][:, 16:20] if via is None else T["rl%d" % t][:, 0:w]
+                tr.append(RemoteDMATransfer(dst_ids=[did(c, core, topo)], dma_engine_mask=m[i], remote_sem=T.sem[("al%d" if via is None else "hl%d") % t],
+                                            src=T["wl%d" % t][:, i * w:(i + 1) * w], dst=out))
+                sent[0] += k
+        else:
+            to = [dst, dst] if via is None else via[:2]
+            srcs = [T["ql%d" % t][:, 0:64].bitcast(dt.uint8), T["sl%d" % t][:, 0:256]]
+            if via is None:
+                outs = [T["lc%d" % t][:, 128:192].bitcast(dt.uint8), T["ls%d" % t][:, 128:384]]
+            else:
+                outs = [T["rc%d" % t][:, 0:64].bitcast(dt.uint8), T["rs%d" % t][:, 0:256]]
+            for i, c in enumerate(to):
+                m, k = masks(core, c, 2, topo)
+                tr.append(RemoteDMATransfer(dst_ids=[did(c, core, topo)], dma_engine_mask=m[i], remote_sem=T.sem[("ad%d" if via is None else "hd%d") % t],
+                                            src=srcs[i], dst=outs[i]))
+                sent[0] += k
+        g.remote_dma_fused(tr, local_sem=T.sem.out)
+
+    def issue(q, c):
+        k = c[0]
+        if k == "ts":
+            if c[6] is None:
+                return q.tensor_scalar(ap(c[1]), ap(c[2]), ap(c[3]), None, c[5])
+            return q.tensor_scalar(ap(c[1]), ap(c[2]), ap(c[3]), ap(c[4]), c[5], c[6])
+        if k == "tt":
+            return q.tensor_tensor(ap(c[1]), ap(c[2]), ap(c[3]), c[4])
+        if k == "scan":
+            return q.tensor_tensor_scan(ap(c[1]), ap(c[2]), ap(c[3]), ap(c[4]), c[5], c[6])
+        if k == "copy":
+            return q.tensor_copy(ap(c[1]), ap(c[2]))
+        if k == "memset":
+            return q.memset(ap(c[1]), c[2])
+        if k == "red":
+            return q.tensor_reduce(ap(c[1]), ap(c[2]), AxisListType.X, A.add)
+        if k == "act":
+            if c[6] is not None:
+                return q.activation(ap(c[1]), ap(c[2]), c[3], bias=ap(c[4]), scale=c[5], accum_out=ap(c[6]))
+            if c[4] != 0.0 or c[3] != F.Identity:
+                return q.activation(ap(c[1]), ap(c[2]), c[3], bias=ap(c[4]), scale=c[5])
+            return q.activation(ap(c[1]), ap(c[2]), F.Copy, scale=c[5])
+        if k == "plane":
+            return q.activation(ap(c[1]), ap(c[2]), F.Copy)
+        if k == "quant":
+            return q.quantize_mx(ap(c[1]), ap(c[2]), ap(c[3]))
+        if k == "mm":
+            return q.matmul_mx(ap(c[1]), ap(c[2]), ap(c[3]), ap(c[4]), ap(c[5]), c[6], c[7])
+        if k == "pick":
+            return q.tensor_copy(ap(c[1]).bitcast(dt.uint32), ap(c[2]).bitcast(dt.uint32).indirect(ap(c[3])))
+        if k == "iota":
+            if DTYPE[c[1][0]] == i32:
+                return q.iota(ap(c[1]), c[2], c[3], c[4])
+            return q.iota(ap(c[1]), c[2], c[3], c[4], allow_small_or_imprecise_dtypes=True)
+        if k == "sel":
+            return q.affine_select(ap(c[1]), ap(c[2]), c[3], A.is_equal, 0.0, c[4], c[5])
+        if k == "load":
+            out = T[c[1]][:]
+            return q.dma_start(out.bitcast(dt.uint8) if DTYPE[c[1]] == q8 else out, T[c[2]][:])
+        if k == "move":
+            return q.dma_start(ap(c[1]), ap(c[2]))
+        if k == "codes":
+            return q.dma_start(T.oc[:, 4 * c[1]:4 * c[2]], T.qx3[:, c[1]:c[2]].bitcast(dt.uint8))
+        if k == "scales":
+            return q.dma_start(T.osc[4 * c[1]:4 * c[1] + 4, 0:C], T.sx3[32 * c[1]:32 * c[1] + 4, 0:C])
+        if k == "y":
+            return q.dma_start(T.y[:, c[1]:c[2]], T.yb[:, c[1]:c[2]])
+        if k == "ot":
+            return q.dma_start(T.ot[:, :], T.otb[0:128:16, 0:C])
+
+    mark = {}
+    count = {e: 0 for e in "VSPG"}
+    ndma = [0]
+    for i in order:
+        o = ops[i]
+        if o.get("arrival"):
+            mark[i] = (o["arrival"], arrivals(int(o["arrival"][2:]))[0 if o["arrival"][1] == "l" else 1])
+        elif o.get("send"):
+            mark[i] = None
+        elif o.get("dma"):
+            mark[i] = ("d%d" % ndma[0], 16)
+            ndma[0] += 1
+        else:
+            count[o["eng"]] += sum(1 for c in o["call"][1] if c) if o["call"][0] == "multi" else 1
+            mark[i] = (o["eng"], count[o["eng"]])
+    seen = {}
+    for i in order:
+        o = ops[i]
+        e = o["eng"]
+        if e == "N":
+            continue
+        q = queue[e]
+        need = {}
+        for j in o["deps"]:
+            if mark[j] is None or (o.get("acc") and ops[j]["eng"] == "P"):
+                continue
+            s, k = mark[j]
+            need[s] = max(need.get(s, 0), k)
+        for s, k in need.items():
+            if seen.get((e, s), 0) < k:
+                q.wait_ge(T.sem[s], k)
+                seen[(e, s)] = k
+        if o.get("send"):
+            send(o["call"][0], o["call"][1])
+        elif o["call"][0] == "multi":
+            k = mark[i][1] - sum(1 for c in o["call"][1] if c)
+            for c in o["call"][1]:
+                if c:
+                    issue(q, c).then_inc(T.sem[e], 1)
+                    k += 1
+                else:
+                    q.wait_ge(T.sem[e], k)
+                    seen[(e, e)] = k
+        else:
+            issue(q, o["call"]).then_inc(T.sem[mark[i][0]], 16 if o.get("dma") else 1)
+    ends = {}
+    for m in mark.values():
+        if m is not None:
+            ends[m[0]] = max(ends.get(m[0], 0), m[1])
+    ends["out"] = sent[0]
+    for s, k in ends.items():
+        if max([c for (e, s2), c in seen.items() if s2 == s] + [0]) < k:
+            g.sync.wait_ge(T.sem[s], k)

@@ -18,16 +18,17 @@ PER = {"s": (320, f32), "tie": (320, f32), "dd": (320, f32), "nu": (320, b16), "
        "H": (4 * HW, b16), "E": (1280, b16), "fl": (176, b16), "nst": (8, f32), "lu": (320, b16), "luT": (320, b16),
        "luN": (320, b16), "cl": (320, b16), "cs": (320, b16), "clT": (320, b16), "csT": (320, b16), "lw": (64, f32),
        "slw": (64, f32), "twn": (256, f32), "stw": (256, f32), "qz": (176, q8), "sz": (176, u8), "qc": (480, q8), "sc": (480, u8)}
-JUNK = {"o0": (0, 10, 176), "op": (1780, 8, 144), "on": (2948, 2, 64), "l": (3080, 4, 320), "q": (4368, 16, 80)}
+JUNK = {"o0": (0, 10, 176), "op": (1780, 8, 144), "on": (2948, 2, 64), "l": (3080, 4, 272), "q": (4368, 16, 80)}
+BATCH = {"o0": 4, "op": 3, "q": 7}
 ONE = {"x0": (1280, b16), "ut": (512, b16), "vt": (512, b16), "twi": (20, i32), "wq": (512, q8), "wp": (512, u8),
        "qu0": (128, q8), "su0": (128, u8), "qu": (128, q8), "su": (128, u8), "qv": (128, q8), "sv": (128, u8),
-       "iota": (320, f32), "iotT": (320, f32), "iotU": (320, f32), "far": (512, f32), "sg": (1600, b16),
-       "j16": (320, f32), "j4": (320, f32), "ge": (512, b16), "pi": (8, i32),
-       "pk": (8, i32), "col": (16, f32), "c16": (20, f32), "kb": (20, f32), "ob": (20, f32), "urep": (8, u16), "blk": (16, u16),
-       "mask": (320, f32), "sel16": (320, f32), "m4": (320, f32), "sel4": (320, f32), "rst": (160, f32), "eps": (160, f32),
+       "iota": (320, f32), "iotT": (640, f32), "far": (1024, f32), "sg": (1600, b16),
+       "j16": (320, f32), "j4": (320, f32), "ge": (512, b16), "sdump": (128, u8),
+       "pk": (8, i32), "col": (16, f32), "c16": (20, f32), "kb": (20, f32), "urep": (8, u16), "blk": (16, u16),
+       "mask": (320, f32), "sel16": (320, f32), "sel4": (320, f32), "rst": (160, f32), "eps": (160, f32),
        "ones": (512, b16), "bd": (512, b16), "qbd": (128, q8), "sbd": (128, u8), "eb": (2048, b16),
        "qe": (512, q8), "se": (512, u8), "zero": (640, b16), "qdump": (128, q8), "CC": (1920, b16), "L": (512, b16),
-       "yb": (320, f32), "otb": (320, f32), "junk": (5680, b16)}
+       "yb": (320, f32), "otb": (320, f32), "junk": (5680, b16), "cap": (3072, b16), "run": (1024, b16), "ob": (80, f32)}
 for _t in range(R + 1):
     ONE["qx%d" % _t] = (320, q8)
     ONE["sx%d" % _t] = (320, u8)
@@ -47,12 +48,12 @@ SCRATCH = {k: ("sbuf", [128, w * R], d) for k, (w, d) in PER.items()}
 SCRATCH.update({k: ("sbuf", [128, w], d) for k, (w, d) in ONE.items()})
 SCRATCH["ps"] = ("psum", [128, 4096], f32)
 DTYPE = {k: v[2] for k, v in SCRATCH.items()}
-NDMA = 24
+NDMA = 36
 SEMAPHORES = (["V", "S", "P", "G", "out"] + ["d%d" % i for i in range(NDMA)] + ["ad%d" % t for t in range(R)]
               + ["al%d" % t for t in range(R)] + ["hd%d" % t for t in range(2)] + ["hl%d" % t for t in range(2)])
 
-LAT, HOP2, HOP1, DMA, GATHER = 80.0, 5000.0, 3000.0, 2200.0, 1.6
-TRIES = 4000
+LAT, HOP2, HOP1, DMA, GATHER = 80.0, 5500.0, 3400.0, 2200.0, 1.6
+TRIES = 15000
 
 
 def route(t, r, T, topo):
@@ -166,7 +167,8 @@ def plan():
             vo = ("ts", out, a, scale, None, A.mult, None)
         else:
             vo = ("ts", out, a, scale, bias, A.mult, A.add)
-        add([("S", scost(a), ("act", out, a, F.Identity, bias, scale, None)), ("V", vcost(out, a), vo)], [a], [out])
+        alts = [("S", scost(a), ("act", out, a, F.Identity, bias, scale, None)), ("V", vcost(out, a), vo)]
+        add(alts[1:] if out[0] == "yb" and out[1] else alts, [a], [out])
 
     def act(out, a, func, bias, scale):
         add([("S", scost(a), ("act", out, a, func, bias, scale, None))], [a, bias], [out])
@@ -191,6 +193,9 @@ def plan():
     def dma(q, kind, reads, writes, *args):
         add([(q, 100.0, (kind,) + args)], reads, writes, dma=True)
 
+    def move(out, a, behind=()):
+        dma("Y", "move", list(behind) + [a], [out], out, a)
+
     def ind(w, o):
         return ("ind", w, o)
 
@@ -200,22 +205,24 @@ def plan():
     dma("Y", "load", [], [v("x0", 0, 1280)], "x0", "x")
     dma("S", "load", [], [v("ut", 0, 512)], "ut", "u")
     dma("S", "load", [], [v("twi", 0, 20)], "twi", "tw")
-    dma("Y", "load", [], [v("wq", 0, 512)], "wq", "wc")
-    dma("Y", "load", [], [v("wp", 0, 512)], "wp", "ws")
-    dma("Y", "load", [], [v("vt", 0, 512)], "vt", "v")
+    first = [v("x0", 0, 1280)]
+    dma("Y", "load", first, [v("wq", 0, 512)], "wq", "wc")
+    dma("Y", "load", first, [v("wp", 0, 512)], "wp", "ws")
+    dma("Y", "load", first, [v("vt", 0, 512)], "vt", "v")
+    pi = v("pk", 4, 5)
     iota(v("c16", 0, 20), [[16, 20]], 0, 0)
-    iota(v("pi", 0, 1), [[1, 1]], 0, 1)
+    iota(pi, [[1, 1]], 0, 1)
     iota(v("iota", 0, 320), [[1, 320]], 0, 0)
     iota(v("j16", 0, 320), [[0, 20], [1, 16]], 0, 0)
     iota(v("j4", 0, 320), [[0, 80], [1, 4]], 0, 0)
     iota(v("ge", 0, 512), [[1, 8], [0, 64]], 0, 0)
-    iota(v("ob", 0, 20), [[32, 20]], 0, 0)
+    iota(v("ob", 48, 68), [[32, 20]], 0, 0)
     copy(v("urep", 0, 8), v("c16", 0, 8))
     ts(v("blk", 0, 10), v("c16", 0, 10), 15.0, None, A.add)
-    ts(v("pk", 0, 1), v("pi", 0, 1), 15, None, A.bitwise_and)
-    ts(v("pk", 1, 2), v("pi", 0, 1), 3, None, A.bitwise_and)
-    ts(v("pk", 2, 3), v("pi", 0, 1), 4, None, A.arith_shift_right)
-    ts(v("pk", 3, 4), v("pi", 0, 1), 2, 3, A.arith_shift_right, A.bitwise_and)
+    ts(v("pk", 0, 1), pi, 15, None, A.bitwise_and)
+    ts(v("pk", 1, 2), pi, 3, None, A.bitwise_and)
+    ts(v("pk", 2, 3), pi, 4, None, A.arith_shift_right)
+    ts(v("pk", 3, 4), pi, 2, 3, A.arith_shift_right, A.bitwise_and)
     copy(v("col", 0, 4), v("pk", 0, 4))
     r_, t_, g_, r4_ = [v("col", i, i + 1) for i in range(4)]
     k16, k16m, k16l, k4 = [v("col", i, i + 1) for i in range(4, 8)]
@@ -226,34 +233,41 @@ def plan():
     ts(k4, r4_, 4.0 * UP, t_, A.mult, A.add)
     lin(k4, k4, 1.0, -12.0 * UP)
     lin(v("iotT", 0, 320), v("iota", 0, 320), TINY)
-    lin(v("iotU", 0, 320), v("iota", 0, 320), TINY)
+    lin(v("iotT", 320, 640), v("iota", 0, 320), TINY)
     ts(v("mask", 0, 320), v("j16", 0, 320), r_, None, A.is_equal)
     lin(v("sel16", 0, 320), v("mask", 0, 320), DOWN, UP)
     act(v("far", 0, 320), v("j4", 0, 320), F.Abs, r4_, -1.0)
-    act(v("m4", 0, 320), v("far", 0, 320), F.Relu, 1.0, -1.0)
-    lin(v("sel4", 0, 320), v("m4", 0, 320), DOWN, UP)
+    act(v("far", 0, 320), v("far", 0, 320), F.Relu, 1.0, -1.0)
+    lin(v("sel4", 0, 320), v("far", 0, 320), DOWN, UP)
     act(v("rst", 0, 160), v("j16", 0, 160), F.Sign, 0.0, 1.0)
     ts(v("eps", 0, 160), v("j16", 0, 160), r_, TINY, A.subtract, A.mult)
-    fill(v("ones", 0, 512), 1.0)
-    fill(v("zero", 0, 640), 0.0)
-    act(v("far", 0, 512), v("ge", 0, 512), F.Abs, g_, -1.0)
-    act(v("bd", 0, 512), v("far", 0, 512), F.Relu, 1.0, -1.0)
+    for out, c in ((v("ones", 0, 512), 1), (v("zero", 0, 640), 0)):
+        add([("V", vc(size(out), 0.5), ("memset", out, float(c))), ("G", 130.0 + 2.0 * size(out), ("iota", out, [[0, size(out)]], c, 0))], [], [out])
+    act(v("far", 512, 1024), v("ge", 0, 512), F.Abs, g_, -1.0)
+    act(v("bd", 0, 512), v("far", 512, 1024), F.Relu, 1.0, -1.0)
     quant(v("qbd", 0, 128), v("sbd", 0, 128), v("bd", 0, 512))
     for b in range(4):
         e = v("eb", 512 * b, 512 * b + 512)
         add([("G", 1200.0, ("sel", e, v("ones", 0, 512), [[-1, 512]], b, 4))], [v("ones", 0, 512)], [e])
-        quant(v("qe", 128 * b, 128 * b + 128), v("se", 128 * b, 128 * b + 128), e)
+    quant(v("qe", 0, 512), v("se", 0, 512), v("eb", 0, 2048))
     for j in range(3):
-        dma("Y", "move", [v("zero", 0, 640)], [v("CC", 640 * j, 640 * j + 640)], v("CC", 640 * j, 640 * j + 640), v("zero", 0, 640))
-    dma("Y", "move", [v("zero", 0, 256)], [v("L", 256, 512)], v("L", 256, 512), v("zero", 0, 256))
+        move(v("CC", 640 * j, 640 * j + 640), v("zero", 0, 640), first)
+    move(v("L", 256, 512), v("zero", 0, 256), first)
     fill(("fl", 0, R * 176, 176), 0.0)
     for b in range(4):
         lin(("Z", 644 + b, R * 656, 656), v("zero", 0, R))
     for k, (at, n, w) in JUNK.items():
-        fill(v("junk", at + w, at + n * (w + 2), w + 2), -float(w))
+        if k in BATCH:
+            z = list(BATCH).index(k)
+            iota(v("cap", 1024 * z, 1024 * z + BATCH[k] * w), [[0, BATCH[k]], [4, w]], 0, 0)
+            iota(v("ob", 16 * z, 16 * z + 16), [[32, 16]], -w, 0)
+        else:
+            fill(v("junk", at + w, at + n * (w + 2), w + 2), -float(w))
+    quant(v("qdump", 0, 128), v("sdump", 0, 128), v("zero", 0, 512))
     for t in range(R):
-        quant(v("lc%d" % t, 0, 128), v("ls%d" % t, 0, 128), v("zero", 0, 512))
-        quant(v("qdump", 0, 128), v("sl%d" % t, 128, 256), v("zero", 0, 512))
+        move(v("lc%d" % t, 64, 128), v("qdump", 0, 64), first)
+        move(v("ls%d" % t, 64, 128), v("sdump", 0, 64), first)
+        move(v("sl%d" % t, 128, 256), v("sdump", 0, 128), first)
     quant(v("qu0", 0, 128), v("su0", 0, 128), v("ut", 0, 512))
     add([("V", 260.0, ("pick", v("qu", 0, 128), v("qu0", 0, 128), v("urep", 0, 8)))], [v("qu0", 0, 128), v("urep", 0, 8)], [v("qu", 0, 128)])
     add([("V", 260.0, ("copy", v("su", 0, 128), ind(v("su0", 0, 128), v("urep", 0, 8)))),
@@ -261,18 +275,32 @@ def plan():
     quant(v("qv", 0, 128), v("sv", 0, 128), v("vt", 0, 512))
     copy(v("tw0", 0, 20), v("twi", 0, 20))
 
-    def count(t, row, kind, c0, base, slide, at, out):
+    def count(t, row, kind, c0, base, at, out):
         j0, n, width = JUNK[kind]
-        for i in range(n):
-            c = c0 + i
-            lo, jk = base + (16 * c if slide else 0), j0 + i * (width + 2)
-            win, j, j1, a, kb = v(row, lo, lo + width, 1, t), v("junk", jk, jk + width), v("junk", jk, jk + width + 1), v("acc", at + i, at + i + 1, 1, t), v("kb", c, c + 1)
-            add([("S", 90.0 + max(64, width), ("act", j, win, F.Sign, kb, -1.0, a)),
-                 ("V", vc(width, 0.5) + LAT + vc(width), ("multi", [("ts", j, win, kb, 2.0, A.is_le, A.mult), None, ("red", a, j1)]))],
-                [win, kb, j1], [j, a])
+        nv = BATCH.get(kind, 0)
         a = v("acc", at, at + n, 1, t)
-        if slide:
-            tt(v("ac2", at, at + n, 1, t), a, v("ob", c0, c0 + n), A.add)
+        if nv:
+            z, m = list(BATCH).index(kind), n - nv
+            for i in range(n):
+                win, j, kb = v(row, 16 * i, 16 * i + width, 1, t), v("junk", j0 + i * width, j0 + (i + 1) * width), v("kb", i, i + 1)
+                if i < m:
+                    a = v("acc", at + i, at + i + 1, 1, t)
+                    add([("S", 90.0 + max(64, width), ("act", j, win, F.Sign, kb, -1.0, a))], [win, kb], [j, a])
+                else:
+                    ts(j, win, kb, 2.0, A.is_le, A.mult)
+            scan(v("run", 0, nv * width), v("cap", 1024 * z, 1024 * z + nv * width), v("junk", j0 + m * width, j0 + n * width), 0.0, A.min, A.add)
+            tt(v("ac2", at + m, at + n, 1, t), v("run", width - 1, nv * width, width), v("ob", 16 * z + m, 16 * z + n), A.add)
+            tt(v("ac2", at, at + m, 1, t), v("acc", at, at + m, 1, t), v("ob", 48, 48 + m), A.add)
+            a = v("ac2", at, at + n, 1, t)
+        for i in range(0 if nv else n):
+            c, jk = c0 + i, j0 + i * (width + 2)
+            lo = base + (16 * c if kind == "l" else 0)
+            win, j, j1, one, kb = v(row, lo, lo + width, 1, t), v("junk", jk, jk + width), v("junk", jk, jk + width + 1), v("acc", at + i, at + i + 1, 1, t), v("kb", c, c + 1)
+            add([("S", 90.0 + max(64, width), ("act", j, win, F.Sign, kb, -1.0, one)),
+                 ("V", vc(width, 0.5) + LAT + vc(width), ("multi", [("ts", j, win, kb, 2.0, A.is_le, A.mult), None, ("red", one, j1)]))],
+                [win, kb, j1], [j, one])
+        if kind == "l":
+            tt(v("ac2", at, at + n, 1, t), a, v("ob", 48, 48 + n), A.add)
             a = v("ac2", at, at + n, 1, t)
         ts(v(out, c0, c0 + n, 1, t), a, 0.5, base + width / 2.0, A.mult, A.add)
 
@@ -297,7 +325,7 @@ def plan():
         w = lambda n: v(n, 0, a1, 1, t)
         held = scores(t, a0, a1, v("qu", 0, 128), v("su", 0, 128), p("s"))
         if t == 0 or a0:
-            tt(p("tie"), ind(v("iotT", 0, 320), tw), v("iotU", a0, a1), A.subtract)
+            tt(p("tie"), ind(v("iotT", 0, 320), tw), v("iotT", 320 + a0, 320 + a1), A.subtract)
         else:
             lin(p("tie"), ind(v("tie", 0, C, 1, t - 1), v("qD", 0, 16, 1, t - 1)))
         halves(t, "sT", w("s"), "tw%d" % t, a0, a1)
@@ -311,9 +339,9 @@ def plan():
     def crossings(t, k0, k1, a1, po, pb):
         n = k1 - k0
         if k0:
-            count(t, "cnt", "on", 8, STAY, False, 8, "oD")
+            count(t, "cnt", "on", 8, STAY, 8, "oD")
         else:
-            count(t, "cnt", "o0" if k1 == M else "op", 0, 0, True, 0, "oD")
+            count(t, "cnt", "o0" if k1 == M else "op", 0, 0, 0, "oD")
         o = v("oD", k0 // 16, k1 // 16, 1, t)
         lin(v("gab", po, po + n, 1, t), ind(v("iota", 0, 320), o))
         lin(v("gab", pb, pb + n, 1, t), ind(v("aT", 0, a1, 1, t), o))
@@ -324,10 +352,12 @@ def plan():
         for i in range(0, n, h):
             lin(v("XO", 4 * (1 + k0 + i), 4 * (1 + k0 + i + h), 1, t), ind(v("x%d" % t, 0, 4 * a1), v("ab4", (po + i) // 4, (po + i + h) // 4, 1, t)), 0.5)
         if k0:
-            lin(v("XA", 4 * (1 + k0), 4 * (1 + k1), 1, t), ind(v("x%d" % t, 0, 4 * a1), v("ab4", po // 4, (po + n) // 4, 1, t)), 0.5)
+            lin(v("XA", 4 * (2 + k0), 4 * (2 + k1), 1, t), ind(v("x%d" % t, 0, 4 * a1), v("ab4", po // 4, (po + n) // 4, 1, t)), 0.5)
+        elif t:
+            move(v("XA", 8, 8 + 4 * n, 1, t), v("XO", 4, 4 + 4 * n, 1, t))
         else:
             for i in (0, n // 2):
-                lin(v("XA", 4 * (1 + i), 4 * (1 + i + n // 2), 1, t), v("XO", 4 * (1 + i), 4 * (1 + i + n // 2), 1, t))
+                lin(v("XA", 4 * (2 + i), 4 * (2 + i + n // 2), 1, t), v("XO", 4 * (1 + i), 4 * (1 + i + n // 2), 1, t))
         dd = ind(v("dd", 0, a1, 1, t), o)
         k = lambda nm: v(nm, k0, k1, 1, t)
         lin(k("dR"), dd)
@@ -335,7 +365,7 @@ def plan():
         scan(k("dsc"), v("rst", k0, k1), k("dm"), 0.0, A.mult, A.max)
         if t == 1 and k0 == 0:
             for j in range(2):
-                lin(v("CC", 640 * j + 512, 640 * j + 640), v("zero", 0, 128))
+                move(v("CC", 640 * j + 512, 640 * j + 640), v("zero", 0, 128))
         for c in range(k0 // 16, k1 // 16):
             own, at = v("dsc", 16 * c + 15, 16 * c + 16, 1, t), 640 * (c // 4) + c % 4
             row, sg = v("dR", 0, k1, 1, t), v("sg", 160 * c, 160 * c + k1)
@@ -362,9 +392,8 @@ def plan():
         tw = v("tw%d" % t, 0, 20)
         x = "x%d" % t
         lin(v("XO", 0, 4, 1, t), v("XO", 640, 644, 1, t))
-        lin(v("XA", 0, 4, 1, t), v("XA", 640, 644, 1, t))
-        for lo, hi in ((0, 128), (128, 160)) if t else ((0, 160),):
-            tt(v("Z", 4 + 4 * lo, 4 + 4 * hi, 1, t), ind(w("XO", 644), v("ab4", (pb + lo) // 4, (pb + hi) // 4, 1, t)), v("XA", 4 * lo, 4 * hi, 1, t), A.add)
+        lin(v("XA", 4, 8, 1, t), v("XA", 644, 648, 1, t))
+        tt(v("Z", 4, 644, 1, t), ind(w("XO", 644), v("ab4", pb // 4, pb // 4 + 40, 1, t)), v("XA", 4, 644, 1, t), A.add)
         lin(v("Z", 0, 4, 1, t), v("Z", 640, 644, 1, t))
         quant(w("qz", 162), w("sz", 162), w("Z", 648))
         for b in range(4):
@@ -372,7 +401,9 @@ def plan():
             lin(v("H", HW * b, HW * b + 161, 1, t), ps(2 + b, 0, 161), 0.03125)
             tt(v("E", 320 * b, 320 * b + 320, 1, t), ind(v("H", HW * b, HW * b + 161, 1, t), w("aD", 20)), v(x, b, 1280, 4), A.add)
         if t == 0:
-            ts(v("fl", 1, 161, 1, t), ps(6, 0, 160), 32.0, None, A.is_lt)
+            out = v("fl", 1, 161, 1, t)
+            add([("S", 225.0, ("act", out, ps(6, 0, 160), F.Sign, 31.5, -1.0, None)),
+                 ("V", 210.0, ("ts", out, ps(6, 0, 160), 32.0, None, A.is_lt, None))], [ps(6, 0, 160)], [out])
         else:
             ts(v("fl", 1, 129, 1, t), ps(6, 0, 128), 32.0, None, A.is_lt)
             add([("V", vc(128), ("red", w("nst", 1), v("fl", 1, 129, 1, t)))], [v("fl", 1, 129, 1, t)], [w("nst", 1)])
@@ -380,7 +411,7 @@ def plan():
         tt(w("lu"), ind(w("fl", 161), w("aD", 20)), w("nu"), A.is_gt)
         halves(t, "luT", w("lu"), "tw%d" % t, 0, C)
         scan(w("cl"), w("luT"), w("lu"), 0.0, A.add, A.add)
-        count(t, "cl", "l", 0, 0, False, 10, "lD")
+        count(t, "cl", "l", 0, 0, 10, "lD")
         l, q = w("lD", 4), w("qD", 16)
         for b in range(4):
             lin(v("L", b, 256, 4), ind(v("E", 320 * b, 320 * b + 320, 1, t), l))
@@ -393,7 +424,7 @@ def plan():
         add([("G", 600.0, ("sendl", t))], [v("wl%d" % t, 0, 4), ("goneD%d" % t, 0, 1, 1)], [("goneL%d" % t, 0, 1, 1)], send=True)
         lin(w("luN"), w("luT"), -1.0, 1.0)
         scan(w("cs"), w("luN"), w("lu"), 0.0, A.add, A.subtract)
-        count(t, "cs", "q", 0, 0, True, 16, "qD")
+        count(t, "cs", "q", 0, 0, 16, "qD")
         nx = "x%d" % (t + 1)
         for b in range(4):
             lin(v(nx, b, 1024, 4), ind(v("E", 320 * b, 320 * b + 320, 1, t), q))
@@ -467,6 +498,7 @@ def schedule(ops):
     extra = [DMA if o.get("dma") else 0.0 for o in ops]
     least = [min(a[1] for a in o["alts"]) for o in ops]
     ends = [i for i, o in enumerate(ops) if o.get("send")]
+    goal = [[i for i, o in enumerate(ops) if o["wr"] and o["wr"][0][:2] == ("cnt", 320 * t + STAY)][0] for t in (1, 2)]
 
     def attempt(weight, bias):
         tail = [0.0] * n
@@ -481,11 +513,16 @@ def schedule(ops):
             for a in o["alts"]:
                 st, pos = at, 0
                 if a[0] != "N":
-                    for b0, b1 in busy[a[0]]:
-                        if st + a[1] <= b0:
-                            break
-                        if b1 > st:
-                            st = b1
+                    line = busy[a[0]]
+                    top = len(line)
+                    while pos < top:
+                        mid = (pos + top) // 2
+                        if line[mid][1] > at:
+                            top = mid
+                        else:
+                            pos = mid + 1
+                    while pos < len(line) and st + a[1] > line[pos][0]:
+                        st = line[pos][1]
                         pos += 1
                 key = st + a[1] + (bias[i] if a[0] == "V" else 0.0)
                 if pick is None or key < pick[0]:
@@ -495,22 +532,25 @@ def schedule(ops):
                 busy[a[0]].insert(pos, (st, st + a[1]))
             done[i] = st + a[1] + extra[i]
             got[i] = (a, st)
-        return max(done) + 0.02 * sum(done[i] for i in ends), got, done
+        return [done[goal[0]] + 0.3 * done[ends[0]], done[goal[1]] + 0.3 * done[ends[2]], max(done)], got, done
 
-    rng = np.random.default_rng(1)
-    weight, bias = np.full(n, 1.5), np.full(n, 300.0)
-    best = now = attempt(weight.tolist(), bias.tolist())
-    for it in range(TRIES):
-        w2, b2 = weight.copy(), bias.copy()
-        k = rng.random(n) < 0.004
-        w2[k] = np.exp(rng.normal(0.7, 0.8, int(k.sum())))
-        k = rng.random(n) < 0.004
-        b2[k] = rng.choice([-500.0, 0.0, 300.0, 1000.0, 5000.0], int(k.sum()))
-        new = attempt(w2.tolist(), b2.tolist())
-        if new[0] <= now[0] + 30.0 * (1.0 - it / TRIES):
-            now, weight, bias = new, w2, b2
-            if new[0] < best[0]:
-                best = new
+    cut = [0, goal[0] - 60, goal[1] - 60, n]
+    rng = np.random.default_rng(2)
+    weight, bias = [1.5] * n, [300.0] * n
+    for stage in range(3):
+        best = now = attempt(weight, bias) + (weight, bias)
+        lo, hi = cut[stage], min(n, cut[stage + 1] + 60)
+        for it in range(TRIES):
+            w2, b2 = list(now[3]), list(now[4])
+            for k in rng.integers(lo, hi, 2).tolist():
+                w2[k] = float(np.exp(rng.normal(0.7, 0.8)))
+            b2[int(rng.integers(lo, hi))] = float(rng.choice([-500.0, 0.0, 300.0, 1000.0, 5000.0]))
+            new = attempt(w2, b2) + (w2, b2)
+            if new[0][stage] <= now[0][stage] + 40.0 * (1.0 - it / TRIES):
+                now = new
+                if new[0][stage] < best[0][stage]:
+                    best = new
+        weight, bias = best[3], best[4]
     for i, o in enumerate(ops):
         a, st = best[1][i]
         o["eng"], o["call"], o["start"], o["end"] = a[0], a[2], st, best[2][i]
@@ -616,6 +656,8 @@ def rank_program(g, core, T, topo):
             out = T[c[1]][:]
             return q.dma_start(out.bitcast(dt.uint8) if DTYPE[c[1]] == q8 else out, T[c[2]][:])
         if k == "move":
+            if DTYPE[c[1][0]] == q8:
+                return q.dma_start(ap(c[1]).bitcast(dt.uint8), ap(c[2]).bitcast(dt.uint8))
             return q.dma_start(ap(c[1]), ap(c[2]))
         if k == "codes":
             return q.dma_start(T.oc[:, 4 * c[1]:4 * c[2]], T.qx3[:, c[1]:c[2]].bitcast(dt.uint8))

import numpy as np
from concourse.bass import DstId, RemoteDMATransfer
from concourse.mybir import dt, AluOpType, AxisListType, ActivationFunctionType

A = AluOpType
F = ActivationFunctionType
C, M, R, STAY, GO = 320, 160, 3, 256, 64
STEP = [1, 2, 4]
TINY = 2.0 ** -120
UP, DOWN = 1024.0, -33792.0
HW = 176
f32, b16, i32, u16, q8, u8 = "float32", "bfloat16", "int32", "uint16", "float8_e4m3fn_x4", "uint8"

PER = {"s": (320, f32), "tie": (320, f32), "dd": (320, f32), "nu": (320, b16), "cnt": (320, b16), "aT": (320, b16),
       "sA": (320, f32), "aD": (32, u16), "acc": (32, f32), "ac2": (32, f32), "oD": (16, u16), "lD": (16, u16),
       "qD": (16, u16), "gab": (320, f32), "sab": (320, f32), "ab4": (80, u16), "dR": (160, f32), "dm": (160, f32),
       "dsc": (160, f32), "df": (160, f32), "XO": (656, b16), "XA": (656, b16), "sT": (320, f32), "Z": (656, b16),
       "H": (4 * HW, b16), "E": (1280, b16), "fl": (176, b16), "nst": (8, f32), "lu": (320, b16), "luT": (320, b16),
       "luN": (320, b16), "cl": (320, b16), "cs": (320, b16), "clT": (320, b16), "csT": (320, b16), "lw": (64, f32),
       "slw": (64, f32), "twn": (256, f32), "stw": (256, f32), "qz": (176, q8), "sz": (176, u8), "qc": (480, q8), "sc": (480, u8)}
JUNK = {"o0": (0, 10, 176), "op": (1780, 8, 144), "on": (2948, 2, 64), "l": (3080, 4, 272), "q": (4368, 16, 80)}
BATCH = {"o0": 4, "op": 3, "q": 7}
ONE = {"x0": (1280, b16), "ut": (512, b16), "vt": (512, b16), "twi": (20, i32), "wq": (512, q8), "wp": (512, u8),
       "qu0": (128, q8), "su0": (128, u8), "qu": (128, q8), "su": (128, u8), "qv": (128, q8), "sv": (128, u8),
       "iota": (320, f32), "iotT": (640, f32), "far": (1024, f32), "sg": (1600, b16),
       "j16": (320, f32), "j4": (320, f32), "ge": (512, b16), "sdump": (128, u8),
       "pk": (8, i32), "col": (16, f32), "c16": (20, f32), "kb": (20, f32), "urep": (8, u16), "blk": (16, u16),
       "mask": (320, f32), "sel16": (320, f32), "sel4": (320, f32), "rst": (160, f32), "eps": (160, f32),
       "ones": (512, b16), "bd": (512, b16), "qbd": (128, q8), "sbd": (128, u8), "eb": (2048, b16),
       "qe": (512, q8), "se": (512, u8), "zero": (640, b16), "qdump": (128, q8), "CC": (1920, b16), "L": (512, b16),
       "yb": (320, f32), "otb": (320, f32), "junk": (5680, b16), "cap": (3072, b16), "run": (1024, b16), "ob": (80, f32)}
for _t in range(R + 1):
    ONE["qx%d" % _t] = (320, q8)
    ONE["sx%d" % _t] = (320, u8)
    ONE["tw%d" % _t] = (32, u16)
for _t in range(R):
    ONE["x%d" % (_t + 1)] = (1280, b16)
    ONE["ql%d" % _t] = (128, q8)
    ONE["sl%d" % _t] = (256, u8)
    ONE["wl%d" % _t] = (8, u16)
    ONE["lc%d" % _t] = (192, q8)
    ONE["ls%d" % _t] = (384, u8)
for _t in range(2):
    ONE["rc%d" % _t] = (64, q8)
    ONE["rs%d" % _t] = (256, u8)
    ONE["rl%d" % _t] = (8, u16)
SCRATCH = {k: ("sbuf", [128, w * R], d) for k, (w, d) in PER.items()}
SCRATCH.update({k: ("sbuf", [128, w], d) for k, (w, d) in ONE.items()})
SCRATCH["ps"] = ("psum", [128, 4096], f32)
DTYPE = {k: v[2] for k, v in SCRATCH.items()}
NDMA = 36
SEMAPHORES = (["V", "S", "P", "G", "out"] + ["d%d" % i for i in range(NDMA)] + ["ad%d" % t for t in range(R)]
              + ["al%d" % t for t in range(R)] + ["hd%d" % t for t in range(2)] + ["hl%d" % t for t in range(2)])

LAT, HOP2, HOP1, DMA, GATHER = 80.0, 5500.0, 3400.0, 2200.0, 1.6
TRIES = 15000


def route(t, r, T, topo):
    n = len(T.cores)
    src, dst = T.cores[r], T.cores[(r + STEP[t]) % n]
    if topo.may_write(src, dst):
        return dst, None
    can = [c for c in topo.cores_of(src) if T.rank_of(c) is None and topo.may_write(c, dst)]
    near = [c for c in can if topo.die(c) == topo.die(src)]
    far = [c for c in can if topo.die(c) != topo.die(src)]
    alone = all(topo.may_write(c, T.cores[(T.rank_of(c) + STEP[t]) % n]) for c in topo.cores_of(src) if c != src and T.rank_of(c) is not None)
    return dst, (near[0], near[1], far[:2] if alone else [near[1]])


def masks(src, dst, parts, topo):
    e = topo.engines(src, dst)
    k = len(e) // parts
    return [sum(1 << x for x in e[i * k:(i + 1) * k]) for i in range(parts)], k


def did(dst, src, topo):
    rid, pid = topo.addr(dst, src)
    return DstId(rid=rid, pnc=pid)


def relay_program(g, core, T, topo):
    total = 0
    for t in range(2):
        for r in range(len(T.cores)):
            dst, via = route(t, r, T, topo)
            if via is None or (core not in via[:2] and core not in via[2]):
                continue
            src = T.cores[r]
            rid, pid = topo.addr(dst, core)
            m, k = masks(core, dst, 1, topo)
            if core in via[:2]:
                g.wait_ge(T.sem["hd%d" % t], masks(src, core, 2, topo)[1])
                if core == via[0]:
                    g.remote_dma(T["lc%d" % t][:, 128:192].bitcast(dt.uint8), T["rc%d" % t][:, 0:64].bitcast(dt.uint8), T.sem["ad%d" % t], T.sem.out, pid, rid, m[0])
                else:
                    g.remote_dma(T["ls%d" % t][:, 128:192], T["rs%d" % t][:, 0:64], T.sem["ad%d" % t], T.sem.out, pid, rid, m[0])
                total += k
            if core in via[2]:
                w = 4 // len(via[2])
                i = via[2].index(core)
                g.wait_ge(T.sem["hl%d" % t], masks(src, core, len(via[2]), topo)[1])
                g.remote_dma(T["tw%d" % (t + 1)][:, 16 + i * w:16 + (i + 1) * w], T["rl%d" % t][:, 0:w], T.sem["al%d" % t], T.sem.out, pid, rid, m[0])
                total += k
    if total:
        g.wait_ge(T.sem.out, total)


def plan():
    ops = []

    def v(name, lo, hi, step=1, t=None):
        if name in PER:
            lo, hi = lo + t * PER[name][0], hi + t * PER[name][0]
        return (name, lo, hi, step)

    def size(a):
        if a[0] == "ind":
            return 16 * (a[2][2] - a[2][1])
        return len(range(a[1], a[2], a[3]))

    def regs(xs):
        out = []
        for a in xs:
            if not isinstance(a, tuple):
                continue
            if a[0] == "ind":
                out += [a[1], a[2]]
            else:
                out.append(a)
        return out

    def add(alts, reads, writes, **kw):
        rd, wr = [], list(regs(writes))
        for a in regs(reads):
            (wr if a[0] == "ps" else rd).append(a)
        wr = [("ps", a[1] // 512 * 512, (a[2] + 511) // 512 * 512, 1) if a[0] == "ps" else a for a in wr]
        ops.append(dict(alts=alts, rd=rd, wr=wr, **kw))

    def two(*xs):
        return all(DTYPE[a[0]] in (b16, u16) for a in xs)

    def vc(n, c=1.0):
        return 50.0 + max(64.0, n * c)

    def vcost(out, a, c=1.0):
        if a[0] == "ind":
            return 50.0 + GATHER * size(a)
        return vc(size(a), c * (0.5 if two(out, a) else 1.0))

    def scost(a):
        return 65.0 + (GATHER * size(a) if a[0] == "ind" else max(64.0, size(a)))

    def ts(out, a, s1, s2, op0, op1=None):
        add([("V", vcost(out, a), ("ts", out, a, s1, s2, op0, op1))], [a, s1, s2], [out])

    def tt(out, a, b, op):
        add([("V", vcost(out, a, 1.0 if b[0] == "ps" else 2.0), ("tt", out, a, b, op))], [a, b], [out])

    def scan(out, a, b, init, op0, op1):
        add([("V", vc(size(a), 0.5 if two(out, a, b) else 1.0), ("scan", out, a, b, init, op0, op1))], [a, b, init], [out])

    def lin(out, a, scale=1.0, bias=0.0):
        if scale == 1.0 and bias == 0.0:
            vo = ("copy", out, a)
        elif bias == 0.0:
            vo = ("ts", out, a, scale, None, A.mult, None)
        else:
            vo = ("ts", out, a, scale, bias, A.mult, A.add)
        alts = [("S", scost(a), ("act", out, a, F.Identity, bias, scale, None)), ("V", vcost(out, a), vo)]
        add(alts[1:] if out[0] == "yb" and out[1] else alts, [a], [out])

    def act(out, a, func, bias, scale):
        add([("S", scost(a), ("act", out, a, func, bias, scale, None))], [a, bias], [out])

    def copy(out, a):
        add([("V", vcost(out, a), ("copy", out, a))], [a], [out])

    def fill(out, c):
        add([("V", vc(size(out), 0.5 if two(out) else 1.0), ("memset", out, c))], [], [out])

    def quant(q, s, a):
        add([("V", 50.0 + 0.22 * size(a), ("quant", q, s, a))], [a], [q, s])

    def mm(bank, w, wsc, x, xsc, start=True, stop=True):
        n = size(x)
        out = ("ps", 512 * bank, 512 * bank + n, 1)
        add([("P", 60.0 + 0.7 * (n + 16), ("mm", out, w, wsc, x, xsc, start, stop))], [w, wsc, x, xsc], [out], acc=not start)

    def iota(out, pattern, base, cm):
        add([("G", 130.0 + 2.0 * size(out), ("iota", out, pattern, base, cm))], [], [out])

    def dma(q, kind, reads, writes, *args):
        add([(q, 100.0, (kind,) + args)], reads, writes, dma=True)

    def move(out, a, behind=()):
        dma("Y", "move", list(behind) + [a], [out], out, a)

    def ind(w, o):
        return ("ind", w, o)

    def ps(bank, lo, hi, step=1):
        return ("ps", 512 * bank + lo, 512 * bank + hi, step)

    dma("Y", "load", [], [v("x0", 0, 1280)], "x0", "x")
    dma("S", "load", [], [v("ut", 0, 512)], "ut", "u")
    dma("S", "load", [], [v("twi", 0, 20)], "twi", "tw")
    first = [v("x0", 0, 1280)]
    dma("Y", "load", first, [v("wq", 0, 512)], "wq", "wc")
    dma("Y", "load", first, [v("wp", 0, 512)], "wp", "ws")
    dma("Y", "load", first, [v("vt", 0, 512)], "vt", "v")
    pi = v("pk", 4, 5)
    iota(v("c16", 0, 20), [[16, 20]], 0, 0)
    iota(pi, [[1, 1]], 0, 1)
    iota(v("iota", 0, 320), [[1, 320]], 0, 0)
    iota(v("j16", 0, 320), [[0, 20], [1, 16]], 0, 0)
    iota(v("j4", 0, 320), [[0, 80], [1, 4]], 0, 0)
    iota(v("ge", 0, 512), [[1, 8], [0, 64]], 0, 0)
    iota(v("ob", 48, 68), [[32, 20]], 0, 0)
    copy(v("urep", 0, 8), v("c16", 0, 8))
    ts(v("blk", 0, 10), v("c16", 0, 10), 15.0, None, A.add)
    ts(v("pk", 0, 1), pi, 15, None, A.bitwise_and)
    ts(v("pk", 1, 2), pi, 3, None, A.bitwise_and)
    ts(v("pk", 2, 3), pi, 4, None, A.arith_shift_right)
    ts(v("pk", 3, 4), pi, 2, 3, A.arith_shift_right, A.bitwise_and)
    copy(v("col", 0, 4), v("pk", 0, 4))
    r_, t_, g_, r4_ = [v("col", i, i + 1) for i in range(4)]
    k16, k16m, k16l, k4 = [v("col", i, i + 1) for i in range(4, 8)]
    ts(v("kb", 0, 20), v("c16", 0, 20), r_, 0.5, A.add, A.add)
    lin(k16, r_, UP, -15.0 * UP)
    lin(k16m, r_, UP, -15.0 * UP - 1.0)
    lin(k16l, r_, UP, -15.0 * UP + STAY - 1.0)
    ts(k4, r4_, 4.0 * UP, t_, A.mult, A.add)
    lin(k4, k4, 1.0, -12.0 * UP)
    lin(v("iotT", 0, 320), v("iota", 0, 320), TINY)
    lin(v("iotT", 320, 640), v("iota", 0, 320), TINY)
    ts(v("mask", 0, 320), v("j16", 0, 320), r_, None, A.is_equal)
    lin(v("sel16", 0, 320), v("mask", 0, 320), DOWN, UP)
    act(v("far", 0, 320), v("j4", 0, 320), F.Abs, r4_, -1.0)
    act(v("far", 0, 320), v("far", 0, 320), F.Relu, 1.0, -1.0)
    lin(v("sel4", 0, 320), v("far", 0, 320), DOWN, UP)
    act(v("rst", 0, 160), v("j16", 0, 160), F.Sign, 0.0, 1.0)
    ts(v("eps", 0, 160), v("j16", 0, 160), r_, TINY, A.subtract, A.mult)
    for out, c in ((v("ones", 0, 512), 1), (v("zero", 0, 640), 0)):
        add([("V", vc(size(out), 0.5), ("memset", out, float(c))), ("G", 130.0 + 2.0 * size(out), ("iota", out, [[0, size(out)]], c, 0))], [], [out])
    act(v("far", 512, 1024), v("ge", 0, 512), F.Abs, g_, -1.0)
    act(v("bd", 0, 512), v("far", 512, 1024), F.Relu, 1.0, -1.0)
    quant(v("qbd", 0, 128), v("sbd", 0, 128), v("bd", 0, 512))
    for b in range(4):
        e = v("eb", 512 * b, 512 * b + 512)
        add([("G", 1200.0, ("sel", e, v("ones", 0, 512), [[-1, 512]], b, 4))], [v("ones", 0, 512)], [e])
    quant(v("qe", 0, 512), v("se", 0, 512), v("eb", 0, 2048))
    for j in range(3):
        move(v("CC", 640 * j, 640 * j + 640), v("zero", 0, 640), first)
    move(v("L", 256, 512), v("zero", 0, 256), first)
    fill(("fl", 0, R * 176, 176), 0.0)
    for b in range(4):
        lin(("Z", 644 + b, R * 656, 656), v("zero", 0, R))
    for k, (at, n, w) in JUNK.items():
        if k in BATCH:
            z = list(BATCH).index(k)
            iota(v("cap", 1024 * z, 1024 * z + BATCH[k] * w), [[0, BATCH[k]], [4, w]], 0, 0)
            iota(v("ob", 16 * z, 16 * z + 16), [[32, 16]], -w, 0)
        else:
            fill(v("junk", at + w, at + n * (w + 2), w + 2), -float(w))
    quant(v("qdump", 0, 128), v("sdump", 0, 128), v("zero", 0, 512))
    for t in range(R):
        move(v("lc%d" % t, 64, 128), v("qdump", 0, 64), first)
        move(v("ls%d" % t, 64, 128), v("sdump", 0, 64), first)
        move(v("sl%d" % t, 128, 256), v("sdump", 0, 128), first)
    quant(v("qu0", 0, 128), v("su0", 0, 128), v("ut", 0, 512))
    add([("V", 260.0, ("pick", v("qu", 0, 128), v("qu0", 0, 128), v("urep", 0, 8)))], [v("qu0", 0, 128), v("urep", 0, 8)], [v("qu", 0, 128)])
    add([("V", 260.0, ("copy", v("su", 0, 128), ind(v("su0", 0, 128), v("urep", 0, 8)))),
         ("S", 270.0, ("plane", v("su", 0, 128), ind(v("su0", 0, 128), v("urep", 0, 8))))], [v("su0", 0, 128), v("urep", 0, 8)], [v("su", 0, 128)])
    quant(v("qv", 0, 128), v("sv", 0, 128), v("vt", 0, 512))
    copy(v("tw0", 0, 20), v("twi", 0, 20))

    def count(t, row, kind, c0, base, at, out):
        j0, n, width = JUNK[kind]
        nv = BATCH.get(kind, 0)
        a = v("acc", at, at + n, 1, t)
        if nv:
            z, m = list(BATCH).index(kind), n - nv
            for i in range(n):
                win, j, kb = v(row, 16 * i, 16 * i + width, 1, t), v("junk", j0 + i * width, j0 + (i + 1) * width), v("kb", i, i + 1)
                if i < m:
                    a = v("acc", at + i, at + i + 1, 1, t)
                    add([("S", 90.0 + max(64, width), ("act", j, win, F.Sign, kb, -1.0, a))], [win, kb], [j, a])
                else:
                    ts(j, win, kb, 2.0, A.is_le, A.mult)
            scan(v("run", 0, nv * width), v("cap", 1024 * z, 1024 * z + nv * width), v("junk", j0 + m * width, j0 + n * width), 0.0, A.min, A.add)
            tt(v("ac2", at + m, at + n, 1, t), v("run", width - 1, nv * width, width), v("ob", 16 * z + m, 16 * z + n), A.add)
            tt(v("ac2", at, at + m, 1, t), v("acc", at, at + m, 1, t), v("ob", 48, 48 + m), A.add)
            a = v("ac2", at, at + n, 1, t)
        for i in range(0 if nv else n):
            c, jk = c0 + i, j0 + i * (width + 2)
            lo = base + (16 * c if kind == "l" else 0)
            win, j, j1, one, kb = v(row, lo, lo + width, 1, t), v("junk", jk, jk + width), v("junk", jk, jk + width + 1), v("acc", at + i, at + i + 1, 1, t), v("kb", c, c + 1)
            add([("S", 90.0 + max(64, width), ("act", j, win, F.Sign, kb, -1.0, one)),
                 ("V", vc(width, 0.5) + LAT + vc(width), ("multi", [("ts", j, win, kb, 2.0, A.is_le, A.mult), None, ("red", one, j1)]))],
                [win, kb, j1], [j, one])
        if kind == "l":
            tt(v("ac2", at, at + n, 1, t), a, v("ob", 48, 48 + n), A.add)
            a = v("ac2", at, at + n, 1, t)
        ts(v(out, c0, c0 + n, 1, t), a, 0.5, base + width / 2.0, A.mult, A.add)

    def scores(t, a0, a1, w, wsc, out):
        e = min(a0, a1 - 128)
        q, s = v("qx%d" % t, e, a1), v("sx%d" % t, e, a1)
        quant(q, s, v("x%d" % t, 4 * e, 4 * a1))
        bank = 1 if a0 else 0
        mm(bank, w, wsc, q, s)
        lin(out, ps(bank, a0 - e, a1 - e))
        return ps(bank, a0 - e, a1 - e)

    def halves(t, out, win, lst, a0, a1):
        mid = a0 + (a1 - a0) // 64 * 32 if a1 - a0 > 64 else a1
        for lo, hi in ((a0, mid), (mid, a1)):
            if hi > lo:
                lin(v(out, lo, hi, 1, t), ind(win, v(lst, lo // 16, hi // 16)))

    def places(t, a0, a1):
        tw = v("tw%d" % t, a0 // 16, a1 // 16)
        p = lambda n: v(n, a0, a1, 1, t)
        w = lambda n: v(n, 0, a1, 1, t)
        held = scores(t, a0, a1, v("qu", 0, 128), v("su", 0, 128), p("s"))
        if t == 0 or a0:
            tt(p("tie"), ind(v("iotT", 0, 320), tw), v("iotT", 320 + a0, 320 + a1), A.subtract)
        else:
            lin(p("tie"), ind(v("tie", 0, C, 1, t - 1), v("qD", 0, 16, 1, t - 1)))
        halves(t, "sT", w("s"), "tw%d" % t, a0, a1)
        tt(p("dd"), p("sT"), held, A.subtract)
        tt(p("nu"), p("dd"), p("tie"), A.is_le)
        scan(p("cnt"), v("ones", a0, a1), p("nu"), v("cnt", a0 - 1, a0, 1, t) if a0 else 0.0, A.add, A.subtract)
        lin(p("aT"), ind(w("cnt"), tw))
        scan(p("sA"), v("sel16", a0, a1), p("cnt"), 0.0, A.add, A.max)
        ts(v("aD", a0 // 16, a1 // 16, 1, t), v("sA", a0 + 15, a1, 16, t), k16, None, A.add)

    def crossings(t, k0, k1, a1, po, pb):
        n = k1 - k0
        if k0:
            count(t, "cnt", "on", 8, STAY, 8, "oD")
        else:
            count(t, "cnt", "o0" if k1 == M else "op", 0, 0, 0, "oD")
        o = v("oD", k0 // 16, k1 // 16, 1, t)
        lin(v("gab", po, po + n, 1, t), ind(v("iota", 0, 320), o))
        lin(v("gab", pb, pb + n, 1, t), ind(v("aT", 0, a1, 1, t), o))
        for lo, wd in ([(min(po, pb), 2 * n)] if k0 else [(po, n), (pb, n)]):
            scan(v("sab", lo, lo + wd, 1, t), v("sel4", 0, wd), v("gab", lo, lo + wd, 1, t), 0.0, A.add, A.max)
            ts(v("ab4", lo // 4, (lo + wd) // 4, 1, t), v("sab", lo + 3, lo + wd, 4, t), 4.0, k4, A.mult, A.add)
        h = n // 4 if n > 64 else n
        for i in range(0, n, h):
            lin(v("XO", 4 * (1 + k0 + i), 4 * (1 + k0 + i + h), 1, t), ind(v("x%d" % t, 0, 4 * a1), v("ab4", (po + i) // 4, (po + i + h) // 4, 1, t)), 0.5)
        if k0:
            lin(v("XA", 4 * (2 + k0), 4 * (2 + k1), 1, t), ind(v("x%d" % t, 0, 4 * a1), v("ab4", po // 4, (po + n) // 4, 1, t)), 0.5)
        elif t:
            move(v("XA", 8, 8 + 4 * n, 1, t), v("XO", 4, 4 + 4 * n, 1, t))
        else:
            for i in (0, n // 2):
                lin(v("XA", 4 * (2 + i), 4 * (2 + i + n // 2), 1, t), v("XO", 4 * (1 + i), 4 * (1 + i + n // 2), 1, t))
        dd = ind(v("dd", 0, a1, 1, t), o)
        k = lambda nm: v(nm, k0, k1, 1, t)
        lin(k("dR"), dd)
        tt(k("dm"), dd, v("mask", k0, k1), A.mult)
        scan(k("dsc"), v("rst", k0, k1), k("dm"), 0.0, A.mult, A.max)
        if t == 1 and k0 == 0:
            for j in range(2):
                move(v("CC", 640 * j + 512, 640 * j + 640), v("zero", 0, 128))
        for c in range(k0 // 16, k1 // 16):
            own, at = v("dsc", 16 * c + 15, 16 * c + 16, 1, t), 640 * (c // 4) + c % 4
            row, sg = v("dR", 0, k1, 1, t), v("sg", 160 * c, 160 * c + k1)
            vo, so, outs = [], [("act", sg, row, F.Sign, own, -1.0, None), None], []
            if c:
                outs.append(v("CC", at, at + 64 * c, 4))
                vo.append(("ts", outs[-1], v("dR", 0, 16 * c, 1, t), own, None, A.is_gt, None))
                so.append(("act", outs[-1], v("sg", 160 * c, 176 * c), F.Relu, 0.0, -1.0, None))
            if 16 * c + 16 < k1:
                outs.append(v("CC", at + 64 * c + 64, at + 4 * k1 - c % 4, 4))
                vo.append(("ts", outs[-1], v("dR", 16 * c + 16, k1, 1, t), own, None, A.is_ge, None))
                so.append(("act", outs[-1], v("sg", 176 * c + 16, 160 * c + k1), F.Sign, 1.0, -1.0, None))
            add([("V", sum(vc(size(x)) for x in outs), ("multi", vo)),
                 ("S", scost(row) + LAT + sum(scost(x) for x in outs), ("multi", so))], [row, own], outs + [sg])
        tt(k("df"), ind(v("dsc", 0, k1, 1, t), v("blk", k0 // 16, k1 // 16)), k("dR"), A.subtract)
        tt(v("CC", 1280 + 4 * k0 + 2, 1280 + 4 * k1, 4), k("df"), v("eps", k0, k1), A.is_lt)
        for j in ([0, 1] if k0 == 0 else []) + ([2] if k1 == M else []):
            q, s = v("qc", 160 * j, 160 * j + 160, 1, t), v("sc", 160 * j, 160 * j + 160, 1, t)
            quant(q, s, v("CC", 640 * j, 640 * j + 640))
            mm(6, v("qbd", 0, 128), v("sbd", 0, 128), q, s, j == 0, j == 2)

    def rest(t, pb):
        w = lambda nm, n=320: v(nm, 0, n, 1, t)
        tw = v("tw%d" % t, 0, 20)
        x = "x%d" % t
        lin(v("XO", 0, 4, 1, t), v("XO", 640, 644, 1, t))
        lin(v("XA", 4, 8, 1, t), v("XA", 644, 648, 1, t))
        tt(v("Z", 4, 644, 1, t), ind(w("XO", 644), v("ab4", pb // 4, pb // 4 + 40, 1, t)), v("XA", 4, 644, 1, t), A.add)
        lin(v("Z", 0, 4, 1, t), v("Z", 640, 644, 1, t))
        quant(w("qz", 162), w("sz", 162), w("Z", 648))
        for b in range(4):
            mm(2 + b, v("wq", 128 * b, 128 * b + 128), v("wp", 128 * b, 128 * b + 128), w("qz", 162), w("sz", 162))
            lin(v("H", HW * b, HW * b + 161, 1, t), ps(2 + b, 0, 161), 0.03125)
            tt(v("E", 320 * b, 320 * b + 320, 1, t), ind(v("H", HW * b, HW * b + 161, 1, t), w("aD", 20)), v(x, b, 1280, 4), A.add)
        if t == 0:
            out = v("fl", 1, 161, 1, t)
            add([("S", 225.0, ("act", out, ps(6, 0, 160), F.Sign, 31.5, -1.0, None)),
                 ("V", 210.0, ("ts", out, ps(6, 0, 160), 32.0, None, A.is_lt, None))], [ps(6, 0, 160)], [out])
        else:
            ts(v("fl", 1, 129, 1, t), ps(6, 0, 128), 32.0, None, A.is_lt)
            add([("V", vc(128), ("red", w("nst", 1), v("fl", 1, 129, 1, t)))], [v("fl", 1, 129, 1, t)], [w("nst", 1)])
            ts(v("fl", 129, 161, 1, t), ps(6, 128, 160), w("nst", 1), 32.0, A.add, A.is_lt)
        tt(w("lu"), ind(w("fl", 161), w("aD", 20)), w("nu"), A.is_gt)
        halves(t, "luT", w("lu"), "tw%d" % t, 0, C)
        scan(w("cl"), w("luT"), w("lu"), 0.0, A.add, A.add)
        count(t, "cl", "l", 0, 0, 10, "lD")
        l, q = w("lD", 4), w("qD", 16)
        for b in range(4):
            lin(v("L", b, 256, 4), ind(v("E", 320 * b, 320 * b + 320, 1, t), l))
        quant(v("ql%d" % t, 0, 128), v("sl%d" % t, 0, 128), v("L", 0, 512))
        add([("G", 600.0, ("sendd", t))], [v("ql%d" % t, 0, 64), v("sl%d" % t, 0, 256)], [("goneD%d" % t, 0, 1, 1)], send=True)
        lin(w("clT"), ind(w("cl"), tw))
        lin(w("lw", 64), ind(w("clT"), l))
        scan(w("slw", 64), v("sel16", 0, 64), w("lw", 64), 0.0, A.add, A.max)
        ts(v("wl%d" % t, 0, 4), v("slw", 15, 64, 16, t), k16l, None, A.add)
        add([("G", 600.0, ("sendl", t))], [v("wl%d" % t, 0, 4), ("goneD%d" % t, 0, 1, 1)], [("goneL%d" % t, 0, 1, 1)], send=True)
        lin(w("luN"), w("luT"), -1.0, 1.0)
        scan(w("cs"), w("luN"), w("lu"), 0.0, A.add, A.subtract)
        count(t, "cs", "q", 0, 0, 16, "qD")
        nx = "x%d" % (t + 1)
        for b in range(4):
            lin(v(nx, b, 1024, 4), ind(v("E", 320 * b, 320 * b + 320, 1, t), q))
        lin(w("csT"), ind(w("cs"), tw))
        lin(w("twn", 256), ind(w("csT"), q))
        scan(w("stw", 256), v("sel16", 0, 256), w("twn", 256), 0.0, A.add, A.max)
        ts(v("tw%d" % (t + 1), 0, 16), v("stw", 15, 256, 16, t), k16m, None, A.add)

    def arrive(t):
        hop = HOP2 if t < 2 else HOP1
        add([("N", hop, None)], [("goneL%d" % t, 0, 1, 1)], [v("tw%d" % (t + 1), 16, 20)], arrival="al%d" % t)
        add([("N", hop, None)], [("goneD%d" % t, 0, 1, 1)], [v("lc%d" % t, 128, 192), v("ls%d" % t, 128, 384)], arrival="ad%d" % t)
        for b in range(4):
            mm(2 + b, v("qe", 128 * b, 128 * b + 128), v("se", 128 * b, 128 * b + 128), v("lc%d" % t, 64, 192), v("ls%d" % t, 64, 192))
            lin(v("x%d" % (t + 1), 1024 + b, 1280, 4), ps(2 + b, 64, 128))

    for t in range(R):
        if t == 0:
            places(t, 0, C)
            crossings(t, 0, M, C, 0, 160)
            rest(t, 160)
        else:
            places(t, 0, STAY)
            crossings(t, 0, 128, STAY, 0, 128)
            arrive(t - 1)
            places(t, STAY, C)
            crossings(t, 128, M, C, 288, 256)
            rest(t, 128)
    qv, sv = v("qv", 0, 128), v("sv", 0, 128)
    scores(R, 0, 192, qv, sv, v("yb", 0, 192))
    dma("Y", "codes", [v("qx3", 0, 192)], [], 0, 192)
    dma("Y", "y", [v("yb", 0, 192)], [], 0, 192)
    arrive(R - 1)
    lin(v("otb", 0, C), ind(v("iota", 0, C), v("tw3", 0, 20)))
    dma("Y", "ot", [v("otb", 0, C)], [])
    scores(R, 192, C, qv, sv, v("yb", 192, C))
    dma("Y", "codes", [v("qx3", 192, C)], [], 192, C)
    for k in range(4):
        dma("SY"[k % 2], "scales", [v("sx3", 0, C)], [], k)
    dma("S", "y", [v("yb", 192, C)], [], 192, C)
    return ops


def meets(a, b):
    if a[0] != b[0] or a[2] <= b[1] or b[2] <= a[1]:
        return False
    if a[3] == b[3] and a[3] > 1:
        return a[1] % a[3] == b[1] % a[3]
    return True


def schedule(ops):
    n = len(ops)
    last = {}
    for i, o in enumerate(ops):
        deps = set()
        for a in o["rd"]:
            deps.update(j for (b, j, wr) in last.get(a[0], []) if wr and meets(a, b))
        for a in o["wr"]:
            deps.update(j for (b, j, wr) in last.get(a[0], []) if meets(a, b))
        deps.discard(i)
        o["deps"] = sorted(deps)
        for a in o["rd"]:
            last.setdefault(a[0], []).append((a, i, False))
        for a in o["wr"]:
            last.setdefault(a[0], []).append((a, i, True))
    after = [[] for _ in range(n)]
    for i, o in enumerate(ops):
        for j in o["deps"]:
            after[j].append(i)
    extra = [DMA if o.get("dma") else 0.0 for o in ops]
    least = [min(a[1] for a in o["alts"]) for o in ops]
    ends = [i for i, o in enumerate(ops) if o.get("send")]
    goal = [[i for i, o in enumerate(ops) if o["wr"] and o["wr"][0][:2] == ("cnt", 320 * t + STAY)][0] for t in (1, 2)]

    def attempt(weight, bias):
        tail = [0.0] * n
        for i in range(n - 1, -1, -1):
            tail[i] = least[i] * weight[i] + extra[i] + max([LAT + tail[j] for j in after[i]] + [0.0])
        busy = {e: [] for e in "VSPGY"}
        done, got = [0.0] * n, [None] * n
        for i in sorted(range(n), key=lambda x: -tail[x]):
            o = ops[i]
            at = max([done[j] + LAT for j in o["deps"]] + [0.0])
            pick = None
            for a in o["alts"]:
                st, pos = at, 0
                if a[0] != "N":
                    line = busy[a[0]]
                    top = len(line)
                    while pos < top:
                        mid = (pos + top) // 2
                        if line[mid][1] > at:
                            top = mid
                        else:
                            pos = mid + 1
                    while pos < len(line) and st + a[1] > line[pos][0]:
                        st = line[pos][1]
                        pos += 1
                key = st + a[1] + (bias[i] if a[0] == "V" else 0.0)
                if pick is None or key < pick[0]:
                    pick = (key, a, st, pos)
            key, a, st, pos = pick
            if a[0] != "N":
                busy[a[0]].insert(pos, (st, st + a[1]))
            done[i] = st + a[1] + extra[i]
            got[i] = (a, st)
        return [done[goal[0]] + 0.3 * done[ends[0]], done[goal[1]] + 0.3 * done[ends[2]], max(done)], got, done

    cut = [0, goal[0] - 60, goal[1] - 60, n]
    rng = np.random.default_rng(2)
    weight, bias = [1.5] * n, [300.0] * n
    for stage in range(3):
        best = now = attempt(weight, bias) + (weight, bias)
        lo, hi = cut[stage], min(n, cut[stage + 1] + 60)
        for it in range(TRIES):
            w2, b2 = list(now[3]), list(now[4])
            for k in rng.integers(lo, hi, 2).tolist():
                w2[k] = float(np.exp(rng.normal(0.7, 0.8)))
            b2[int(rng.integers(lo, hi))] = float(rng.choice([-500.0, 0.0, 300.0, 1000.0, 5000.0]))
            new = attempt(w2, b2) + (w2, b2)
            if new[0][stage] <= now[0][stage] + 40.0 * (1.0 - it / TRIES):
                now = new
                if new[0][stage] < best[0][stage]:
                    best = new
        weight, bias = best[3], best[4]
    for i, o in enumerate(ops):
        a, st = best[1][i]
        o["eng"], o["call"], o["start"], o["end"] = a[0], a[2], st, best[2][i]
    return sorted(range(n), key=lambda i: (ops[i]["start"], i))


PLAN = {}


def rank_program(g, core, T, topo):
    rank = T.rank_of(core)
    if rank is None:
        relay_program(g, core, T, topo)
        return
    if not PLAN:
        PLAN["ops"] = plan()
        PLAN["order"] = schedule(PLAN["ops"])
    ops, order = PLAN["ops"], PLAN["order"]
    n = len(T.cores)
    queue = {"V": g.vector, "S": g.scalar, "P": g.tensor, "G": g, "Y": g.sync}

    def ap(a):
        if not isinstance(a, tuple):
            return a
        if a[0] == "ind":
            return ap(a[1]).indirect(ap(a[2]))
        return T[a[0]][:, a[1]:a[2]] if a[3] == 1 else T[a[0]][:, a[1]:a[2]:a[3]]

    def arrivals(t):
        src_rank = (rank - STEP[t]) % n
        src = T.cores[src_rank]
        via = route(t, src_rank, T, topo)[1]
        if via is None:
            k = len(topo.engines(src, core))
            return k, k
        return sum(len(topo.engines(c, core)) for c in via[2]), sum(len(topo.engines(c, core)) for c in via[:2])

    sent = [0]

    def send(kind, t):
        dst, via = route(t, rank, T, topo)
        tr = []
        if kind == "sendl":
            to = [dst] if via is None else via[2]
            w = 4 // len(to)
            for i, c in enumerate(to):
                m, k = masks(core, c, len(to), topo)
                out = T["tw%d" % (t + 1)][:, 16:20] if via is None else T["rl%d" % t][:, 0:w]
                tr.append(RemoteDMATransfer(dst_ids=[did(c, core, topo)], dma_engine_mask=m[i], remote_sem=T.sem[("al%d" if via is None else "hl%d") % t],
                                            src=T["wl%d" % t][:, i * w:(i + 1) * w], dst=out))
                sent[0] += k
        else:
            to = [dst, dst] if via is None else via[:2]
            srcs = [T["ql%d" % t][:, 0:64].bitcast(dt.uint8), T["sl%d" % t][:, 0:256]]
            if via is None:
                outs = [T["lc%d" % t][:, 128:192].bitcast(dt.uint8), T["ls%d" % t][:, 128:384]]
            else:
                outs = [T["rc%d" % t][:, 0:64].bitcast(dt.uint8), T["rs%d" % t][:, 0:256]]
            for i, c in enumerate(to):
                m, k = masks(core, c, 2, topo)
                tr.append(RemoteDMATransfer(dst_ids=[did(c, core, topo)], dma_engine_mask=m[i], remote_sem=T.sem[("ad%d" if via is None else "hd%d") % t],
                                            src=srcs[i], dst=outs[i]))
                sent[0] += k
        g.remote_dma_fused(tr, local_sem=T.sem.out)

    def issue(q, c):
        k = c[0]
        if k == "ts":
            if c[6] is None:
                return q.tensor_scalar(ap(c[1]), ap(c[2]), ap(c[3]), None, c[5])
            return q.tensor_scalar(ap(c[1]), ap(c[2]), ap(c[3]), ap(c[4]), c[5], c[6])
        if k == "tt":
            return q.tensor_tensor(ap(c[1]), ap(c[2]), ap(c[3]), c[4])
        if k == "scan":
            return q.tensor_tensor_scan(ap(c[1]), ap(c[2]), ap(c[3]), ap(c[4]), c[5], c[6])
        if k == "copy":
            return q.tensor_copy(ap(c[1]), ap(c[2]))
        if k == "memset":
            return q.memset(ap(c[1]), c[2])
        if k == "red":
            return q.tensor_reduce(ap(c[1]), ap(c[2]), AxisListType.X, A.add)
        if k == "act":
            if c[6] is not None:
                return q.activation(ap(c[1]), ap(c[2]), c[3], bias=ap(c[4]), scale=c[5], accum_out=ap(c[6]))
            if c[4] != 0.0 or c[3] != F.Identity:
                return q.activation(ap(c[1]), ap(c[2]), c[3], bias=ap(c[4]), scale=c[5])
            return q.activation(ap(c[1]), ap(c[2]), F.Copy, scale=c[5])
        if k == "plane":
            return q.activation(ap(c[1]), ap(c[2]), F.Copy)
        if k == "quant":
            return q.quantize_mx(ap(c[1]), ap(c[2]), ap(c[3]))
        if k == "mm":
            return q.matmul_mx(ap(c[1]), ap(c[2]), ap(c[3]), ap(c[4]), ap(c[5]), c[6], c[7])
        if k == "pick":
            return q.tensor_copy(ap(c[1]).bitcast(dt.uint32), ap(c[2]).bitcast(dt.uint32).indirect(ap(c[3])))
        if k == "iota":
            if DTYPE[c[1][0]] == i32:
                return q.iota(ap(c[1]), c[2], c[3], c[4])
            return q.iota(ap(c[1]), c[2], c[3], c[4], allow_small_or_imprecise_dtypes=True)
        if k == "sel":
            return q.affine_select(ap(c[1]), ap(c[2]), c[3], A.is_equal, 0.0, c[4], c[5])
        if k == "load":
            out = T[c[1]][:]
            return q.dma_start(out.bitcast(dt.uint8) if DTYPE[c[1]] == q8 else out, T[c[2]][:])
        if k == "move":
            if DTYPE[c[1][0]] == q8:
                return q.dma_start(ap(c[1]).bitcast(dt.uint8), ap(c[2]).bitcast(dt.uint8))
            return q.dma_start(ap(c[1]), ap(c[2]))
        if k == "codes":
            return q.dma_start(T.oc[:, 4 * c[1]:4 * c[2]], T.qx3[:, c[1]:c[2]].bitcast(dt.uint8))
        if k == "scales":
            return q.dma_start(T.osc[4 * c[1]:4 * c[1] + 4, 0:C], T.sx3[32 * c[1]:32 * c[1] + 4, 0:C])
        if k == "y":
            return q.dma_start(T.y[:, c[1]:c[2]], T.yb[:, c[1]:c[2]])
        if k == "ot":
            return q.dma_start(T.ot[:, :], T.otb[0:128:16, 0:C])

    mark = {}
    count = {e: 0 for e in "VSPG"}
    ndma = [0]
    for i in order:
        o = ops[i]
        if o.get("arrival"):
            mark[i] = (o["arrival"], arrivals(int(o["arrival"][2:]))[0 if o["arrival"][1] == "l" else 1])
        elif o.get("send"):
            mark[i] = None
        elif o.get("dma"):
            mark[i] = ("d%d" % ndma[0], 16)
            ndma[0] += 1
        else:
            count[o["eng"]] += sum(1 for c in o["call"][1] if c) if o["call"][0] == "multi" else 1
            mark[i] = (o["eng"], count[o["eng"]])
    seen = {}
    for i in order:
        o = ops[i]
        e = o["eng"]
        if e == "N":
            continue
        q = queue[e]
        need = {}
        for j in o["deps"]:
            if mark[j] is None or (o.get("acc") and ops[j]["eng"] == "P"):
                continue
            s, k = mark[j]
            need[s] = max(need.get(s, 0), k)
        for s, k in need.items():
            if seen.get((e, s), 0) < k:
                q.wait_ge(T.sem[s], k)
                seen[(e, s)] = k
        if o.get("send"):
            send(o["call"][0], o["call"][1])
        elif o["call"][0] == "multi":
            k = mark[i][1] - sum(1 for c in o["call"][1] if c)
            for c in o["call"][1]:
                if c:
                    issue(q, c).then_inc(T.sem[e], 1)
                    k += 1
                else:
                    q.wait_ge(T.sem[e], k)
                    seen[(e, e)] = k
        else:
            issue(q, o["call"]).then_inc(T.sem[mark[i][0]], 16 if o.get("dma") else 1)
    ends = {}
    for m in mark.values():
        if m is not None:
            ends[m[0]] = max(ends.get(m[0], 0), m[1])
    ends["out"] = sent[0]
    for s, k in ends.items():
        if max([c for (e, s2), c in seen.items() if s2 == s] + [0]) < k:
            g.sync.wait_ge(T.sem[s], k)
